import numpy as np, ml_dtypes
CORES = [40,64,80,88,96,104,120,144]
N = 8
BF = ml_dtypes.bfloat16
def gentries(a):
    return np.ascontiguousarray(a.reshape(8, 16, -1).transpose(0, 2, 1)).reshape(8, -1)
def gtable(e):
    e = np.asarray(e); return np.ascontiguousarray(e.reshape(8, -1, 16).transpose(0, 2, 1)).reshape(128, -1).astype(np.int32)
W, L, B, VI, PS, ST = 2048, 12, 256, 4, 5, 8
KAP = 149 * np.arange(L) + 37
def tables_of(rng):
    lv = rng.random((N, 8, 16, W), dtype=np.float32); x = rng.integers(0, 16, (N, 8, 16, W))
    h = rng.choice(np.array([0.15, 0.22, 0.3]), (N, 8, 1, 1)); w = rng.choice(np.array([0.12, 0.18]), (N, 8, 1, 1))
    e = np.where(lv < h, 12 + (x & 3), np.where(lv < h + w, x & 3, 4 + (x & 7)))
    nd = rng.choice(np.array([0.0, 0.05, 0.1, 0.2]), (N, 8, 1, W)); x = rng.integers(0, 12, (N, 8, 16, W))
    return e, np.where(rng.random((N, 8, 16, W), dtype=np.float32) < nd, 12 + (x & 3), x)
def own_steps(rng, s):
    return np.take_along_axis(s, rng.integers(0, L, (N, 8, L, B)), axis=2)
def pack(e, p, s, q, st, th):
    return {"eff": e.reshape(N, 128, W).astype(np.float32).astype(BF), "req": p.reshape(N, 128, W).astype(np.float32).astype(BF),
            "act": np.stack([gtable(a.reshape(8, L * B)) for a in s]), "why": np.stack([gtable(a.reshape(8, L * B)) for a in q]),
            "st0": np.ascontiguousarray(st).reshape(N, 128, B).astype(np.float32).astype(BF), "bar": np.stack([gtable(a) for a in th])}
def setup_inputs(rng):
    e, p = tables_of(rng); s = rng.integers(0, W, (N, 8, L, B)); w = rng.integers(0, 5, (N, 8, L, B))
    q = np.where(w < 2, -1, np.where(w < 4, own_steps(rng, s), rng.integers(0, W, (N, 8, L, B))))
    return pack(e, p, s, q, rng.integers(0, 16, (N, 8, 16, B)), rng.choice(np.array([0, 1, 2, 2, 3, 3, 4]), (N, 8, B)))
def setup_inputs_alike(rng):
    e, p = tables_of(rng)
    fw = np.concatenate([np.argsort(rng.random((N, 8, W - 2)), axis=-1)[..., :4] + 1, np.zeros((N, 8, 1), np.int64), np.full((N, 8, 1), W - 1)], axis=2)
    ix = np.broadcast_to(fw[:, :, None, :], (N, 8, 16, 6))
    np.put_along_axis(e, ix, rng.choice(np.array([0, 3, 4, 8, 11, 12, 15]), (N, 8, 16, 6)), axis=3)
    np.put_along_axis(p, ix, np.where(rng.random((N, 8, 16, 6)) < 0.2, 12, 11), axis=3)
    n = rng.integers(0, 6, (N, 8, L, B)); n[:, 1::2] = n[:, 1::2, :, :1]
    n = np.where(rng.random((N, 8, 1, B)) < 0.15, n[:, :, :1], n)
    s = np.take_along_axis(fw, n.reshape(N, 8, L * B), axis=2).reshape(N, 8, L, B)
    q = np.take_along_axis(fw, rng.integers(0, 6, (N, 8, L * B)), axis=2).reshape(N, 8, L, B)
    q = np.where(rng.random((N, 8, L, B)) < 0.4, -1, q)
    return pack(e, p, s, q, rng.integers(0, 16, (N, 8, 16, B)), rng.integers(0, 5, (N, 8, B)))
def setup_inputs_corners(rng):
    o = np.argsort(rng.random((N, 8, W)), axis=-1); kc = np.zeros((N, 8, W), np.int64)
    np.put_along_axis(kc, o, np.broadcast_to(np.arange(W) & 7, (N, 8, W)), axis=2)
    k4 = kc[:, :, None, :]; bit = rng.integers(0, 2, (N, 8, 16, W)) == 1
    e = np.where(bit, np.array([4, 0, 12, 4, 4, 4, 4, 4])[k4], np.array([11, 3, 15, 11, 11, 11, 11, 11])[k4])
    e = np.where(k4 == 7, np.array([3, 4, 11, 12])[rng.integers(0, 4, (N, 8, 16, W))], e)
    rk = ((2 * rng.integers(0, 8, (N, 8, 1, W)) + 1) * np.arange(16)[None, None, :, None] + rng.integers(0, 16, (N, 8, 1, W))) & 15
    nd = np.where(k4 == 7, rng.integers(0, 4, (N, 8, 1, W)), np.array([0, 0, 0, 1, 2, 3, 16, 0])[k4]); bit = rng.integers(0, 2, (N, 8, 16, W)) == 1
    p = np.where(rk < nd, np.where(bit, 12, 15), np.where(bit, 11, 0))
    tp = rng.integers(0, 8, (N, 8, 1, B)); y = rng.integers(4, 7, (N, 8, 1, B)); v = rng.integers(1, L, (N, 8, 1, B)); kk = np.arange(L)[None, None, :, None]
    j = rng.choice(np.array([0, L // 2, L - 2]), (N, 8, 1, B)); cp = np.zeros((N, 8, L, B), np.int64)
    cp = np.where((tp == 1) & (kk == 0), y, cp)
    cp = np.where((tp == 2) & (kk == j), 1, cp); cp = np.where((tp == 2) & (kk == L - 1), y, cp)
    cp = np.where(tp == 3, 3, cp)
    for a, b in ((L // 3, 4), (L // 2, 5), (L - 1, 6)): cp = np.where((tp == 4) & (kk == a), b, cp)
    cp = np.where(tp == 5, np.where(kk == v, y, 1), cp)
    cp = np.where((tp == 6) & (kk == 0), 2, cp); cp = np.where((tp == 6) & (kk == L - 1), 1, cp)
    cp = np.where(tp == 7, rng.integers(0, 8, (N, 8, L, B)), cp)
    s = np.take_along_axis(o, (8 * rng.integers(0, W // 8, (N, 8, L, B)) + cp).reshape(N, 8, L * B), axis=2).reshape(N, 8, L, B)
    st = np.array([7, 8, 0, 15])[rng.integers(0, 4, (N, 8, 16, B))]
    st = np.where((tp == 1) | (tp == 3) | (tp == 4), 7, np.where(tp == 2, 8, st))
    h = np.where(tp == 2, j, np.where(tp == 5, v - 1, np.where(tp == 4, L // 3, 0))); own = np.take_along_axis(s, h, axis=2)
    qm = rng.integers(0, 4, (N, 8, 1, B))
    q = np.where(qm == 0, -1, np.where(qm == 1, own, np.where(qm == 2, np.where(rng.random((N, 8, L, B)) < 0.5, own, -1), own_steps(rng, s))))
    return pack(e, p, s, q, st, rng.choice(np.array([0, 1, 2, 3, 16]), (N, 8, B)))
def setup_inputs_ends(rng):
    t = W - 1
    e = 15 * (rng.random((N, 8, 16, W), dtype=np.float32) < rng.choice(np.array([0.0, 0.1, 0.5, 0.9, 1.0]), (N, 8, 1, W))).astype(np.int64)
    p = 15 * (rng.random((N, 8, 16, W), dtype=np.float32) < rng.choice(np.array([0.0, 0.0, 0.1, 0.3, 1.0]), (N, 8, 1, W))).astype(np.int64)
    kk = np.arange(L)[None, None, :, None]; x = rng.choice(np.array([0, 1, L // 2, L - 2, L - 1, L]), (N, 8, 1, B)); x[..., B - 1] = L - 2; x[..., B - 2] = L - 1
    m = rng.random((N, 8, 1, B)) < 0.6; m[..., B - 2:] = True
    s = t * np.where(m, (kk >= x).astype(np.int64), rng.integers(0, 2, (N, 8, L, B)))
    q = np.where(rng.random((N, 8, L, B)) < rng.choice(np.array([0.0, 0.2, 0.5, 1.0]), (N, 8, 1, B)), t, -1)
    st = 15 * (rng.random((N, 8, 16, B)) < rng.choice(np.array([0.0, 0.5, 1.0]), (N, 8, 1, B))).astype(np.int64)
    th = 16 * rng.integers(0, 2, (N, 8, B)); th[..., B - 1] = 16; th[..., B - 2] = 0
    c0 = (KAP * t) & t; c1 = ((t * t >> 5) + KAP * t) & t
    for r in range(N):
        for g in range(8):
            k = (N + 7 - r - g) & 3; u = e[r, g]
            if k == 3: continue
            if k == 0:
                u[0, c0] = 0; u[:, c0[L - 1]] = 15; u[:, 0] = 0; u[:, t] = 15 * rng.integers(0, 2, 16)
            elif k == 1:
                u[:, c1[[1, 2, L - 1]]] = 15; u[5, c1[0]] = 0; u[:, 0] = 15; u[:, t] = 0
            else:
                u[:, c1] = 0; u[:, 0] = 15; u[:, t] = 15; u[rng.permutation(16)[:2], t] = 0
            p[r, g, :, 0] = 0; p[r, g, :, t] = 15
    return pack(e, p, s, q, st, th)
def setup_inputs_full(rng):
    e, p = tables_of(rng); s = rng.integers(0, W, (N, 8, L, B)); st = rng.integers(0, 16, (N, 8, 16, B)); th = rng.choice(np.array([0, 1, 2, 2, 3, 3, 4]), (N, 8, B)); kk = np.arange(L)[:, None]
    for r in range(N):
        for g in range(8):
            m = (g + r + 2 - N) & 7
            if m > 4: continue
            o = rng.permutation(W).reshape(32, W // 32); kc = np.zeros(W, np.int64); kc[o] = np.arange(32)[:, None]
            y = rng.integers(0, 4, (16, W)); e[r, g] = np.where(kc < 17, rng.integers(4, 12, (16, W)), np.where(kc < 20, y, 12 + y))
            rk = ((2 * rng.integers(0, 8, W) + 1) * np.arange(16)[:, None] + rng.integers(0, 16, W)) & 15
            p[r, g] = np.where((rk < kc) & (kc < 17), rng.integers(12, 16, (16, W)), rng.integers(0, 12, (16, W)))
            n = rng.integers(2, 16, B) if m == 0 else rng.integers(4, 17, B)
            x = rng.choice(np.array([0, L // 2, L - 1, L - 1]), B); j = rng.integers(0, L, B); low = (j < x) & (rng.random(B) < 0.5)
            calm = rng.random(B) < (0.1 if m else 0.0)
            if m: calm[B // 2] = True
            kd = np.where(kk == x, n, np.where(kk > x, rng.integers(0, 32, (L, B)), 0)); kd = np.where((kk == j) & low, rng.integers(17, 20, B), kd); kd = np.where(calm, 0, kd)
            s[r, g] = o[kd, rng.integers(0, W // 32, (L, B))]
            st[r, g] = rng.integers(0, 8, (16, B)) + 8 * (low | calm).astype(np.int64)
            up = np.ones(B, np.int64) if m == 0 else rng.integers(0, 2, B)
            th[r, g] = np.minimum(n + up, 16)
    w = rng.integers(0, 5, (N, 8, L, B))
    q = np.where(w < 2, -1, np.where(w < 4, own_steps(rng, s), rng.integers(0, W, (N, 8, L, B))))
    return pack(e, p, s, q, st, th)
def setup_inputs_spread(rng):
    def power(hi, pw, shape): return np.minimum((hi * rng.random(shape, dtype=np.float32) ** pw.astype(np.float32)).astype(np.int64), hi - 1)
    e = power(16, rng.choice(np.array([0.5, 1.0, 2.0]), (N, 8, 16, 1)), (N, 8, 16, W))
    p = power(16, rng.choice(np.array([1.0, 3.0, 8.0, 20.0, 20.0]), (N, 8, 1, W)), (N, 8, 16, W))
    s = power(W, rng.choice(np.array([0.25, 1.0, 4.0]), (N, 8, L, 1)), (N, 8, L, B))
    q = np.where(rng.random((N, 8, L, B)) < 0.5, own_steps(rng, s), rng.integers(-1, W, (N, 8, L, B)))
    return pack(e, p, s, q, power(16, rng.choice(np.array([0.3, 1.0, 3.0]), (N, 8, 1, B)), (N, 8, 16, B)), power(17, rng.choice(np.array([1.0, 3.0, 6.0]), (N, 8, 1)), (N, 8, B)))
def check_inputs(d):
    bad = []
    for k, lo, hi in (("eff", 0, 15), ("req", 0, 15), ("act", 0, W - 1), ("why", -1, W - 1), ("st0", 0, 15), ("bar", 0, 16)):
        v = np.asarray(d[k]).astype(np.float64)
        if not (np.min(v) >= lo and np.max(v) <= hi): bad.append("range of " + k)
        elif np.any(v != np.floor(v)): bad.append("whole numbers in " + k)
    return bad
def pick(tab, ix):
    return np.stack([tab[g][:, ix[g]] for g in range(8)])
def visit(E, P, S, Q, s, th, R, t):
    kk = np.arange(L)[None, :, None]
    es = pick(E, S.reshape(8, L * B)).reshape(8, 16, L, B); ps = pick(P, S.reshape(8, L * B)).reshape(8, 16, L, B)
    flaw = np.zeros((8, 16, L, B), bool)
    for k in range(L):
        flaw[:, :, k] = (ps[:, :, k] >= 12) & (s < 8)
        s = np.where((es[:, :, k] >= 12) | (es[:, :, k] <= 3), es[:, :, k], s)
    over = np.add.reduce(flaw.astype(np.int16), axis=1) >= 2 + (R & 1)
    found = np.any(over, axis=1); ks = np.argmax(over, axis=1)
    fl = np.take_along_axis(flaw, ks[:, None, None, :], 2); need = np.take_along_axis(ps, ks[:, None, None, :], 2) >= 12
    low = np.any((es <= 3) & fl, axis=1) & (kk < ks[:, None, :])
    d = np.where(np.any(low, axis=1), L - 1 - np.argmax(low[:, ::-1], axis=1), ks)
    a = np.take_along_axis(S, ks[:, None, :], 1); z = np.take_along_axis(S, d[:, None, :], 1)
    c = ((a * z >> 5) + KAP[None, :, None] * a + 97 * t) & (W - 1)
    ec = pick(E, c.reshape(8, L * B)).reshape(8, 16, L, B)
    score = np.add.reduce(((ec >= 12) & fl).astype(np.int64), axis=1) - np.add.reduce(((ec <= 3) & need & ~fl).astype(np.int64), axis=1)
    m = np.argmax(score, axis=1); best = np.max(score, axis=1); cm = np.take_along_axis(c, m[:, None, :], 1)
    put = (found & (best >= th))[:, None, :]; ret = (found & (best < th))[:, None, :]
    kb = ks[:, None, :]
    si = np.where(kk < kb, S, np.where(kk == kb, cm, np.concatenate([S[:, :1], S[:, :-1]], axis=1)))
    qi = np.where(kk < kb, Q, np.where(kk == kb, z, np.concatenate([Q[:, :1], Q[:, :-1]], axis=1)))
    go = (kk == d[:, None, :]) | (Q == z)
    order = np.argsort(go, axis=1, kind="stable"); kept = kk < L - np.add.reduce(go.astype(np.int64), axis=1)[:, None, :]
    sr = np.where(kept, np.take_along_axis(S, order, 1), c); qr = np.where(kept, np.take_along_axis(Q, order, 1), -1)
    at = ST * np.arange(B)[None, :] + (np.add.reduce(s.astype(np.int64), axis=1) & (ST - 1))
    e2 = np.array(E); np.put_along_axis(e2, np.broadcast_to(at[:, None, :], (8, 16, B)), (pick(E, at) + s) >> 1, axis=2)
    return np.where(put, si, np.where(ret, sr, S)), np.where(put, qi, np.where(ret, qr, Q)), s, e2, int(np.count_nonzero(ret))
def reference(eff, req, act, why, st0, bar):
    E = [x.astype(np.float32).astype(np.int16).reshape(8, 16, W) for x in eff]; P = [x.astype(np.float32).astype(np.int16).reshape(8, 16, W) for x in req]
    S = [gentries(x).astype(np.int64).reshape(8, L, B) for x in act]; Q = [gentries(x).astype(np.int64).reshape(8, L, B) for x in why]
    s = [x.astype(np.float32).astype(np.int16).reshape(8, 16, B) for x in st0]; th = [gentries(x).astype(np.int64) for x in bar]; R = [0] * N
    for t in range(VI):
        v = [visit(E[r], P[r], S[r], Q[r], s[r], th[r], R[r], t) for r in range(N)]
        E = [x[3] for x in v]; R = [x[4] for x in v]; go = PS if t < VI - 1 else 0
        S = [v[(r - go) % N][0] for r in range(N)]; Q = [v[(r - go) % N][1] for r in range(N)]; s = [v[(r - 1) % N][2] for r in range(N)]
    return {"ys": np.stack([gtable(x.reshape(8, L * B)) for x in S]).astype(np.float32), "yw": np.stack([gtable(x.reshape(8, L * B)) for x in Q]).astype(np.float32),
            "ye": np.stack([x.reshape(128, W) for x in E]).astype(np.float32).astype(BF)}

@@ -1,0 +1,588 @@
+import math
+import numpy as np
+from concourse.mybir import AluOpType as A, ActivationFunctionType as F
+
+N, W, L, VI = 8, 2048, 12, 4
+PLAN_STEP, STATE_STEP = 5, 1
+KAP = [149 * m + 37 for m in range(L)]
+NX = 13 * 256
+ND0, NDO = 98304.0, 248.5
+KZ = -3064.5 - ND0 - 130.0
+LNB = 9 * math.log(2.0)
+THR0 = 16 * ND0
+
+BUFS = {"bfloat16": {}, "float32": {}, "int32": {}, "uint16": {}}
+ARENA = {"bfloat16": {}, "float32": {}, "int32": {}, "uint16": {}}
+for _n in "E X8 PT t120 e8 qa mm nb0 sel sels".split():
+    BUFS["bfloat16"][_n] = W
+for _n in "Gb NB ST".split():
+    BUFS["bfloat16"][_n] = NX
+for _n in "Yb eg yc ng".split():
+    BUFS["bfloat16"][_n] = 3072
+for _n in "ones idn bd1 bd i4k i64k i249 c512".split():
+    BUFS["bfloat16"][_n] = 128
+BUFS["float32"]["ND"] = W
+for _n, _w in (("actl", 192), ("whyl", 192), ("barl", 16)):
+    BUFS["int32"][_n] = _w
+BUFS["bfloat16"]["stl"] = 256
+BUFS["float32"]["ysf"] = BUFS["float32"]["ywf"] = 192
+for _n in "c0t c8t wx sfin enb en u8 uq um uh".split():
+    ARENA["bfloat16"][_n] = 256
+for _n, _w in (("cm15", 64), ("go", 192), ("xkb", 16), ("dkb", 16), ("put", 16), ("ret", 16), ("rj", 16), ("rcb", 16)):
+    ARENA["bfloat16"][_n] = _w
+for _n in "SF QF".split():
+    ARENA["float32"][_n] = 192
+for _n in ("ki ckx ckd ckm KX KD kk am dk0 kadd goq zs zq tlc dr dr0 drq dis diq eqm gt gem c1 na nc qa1 qc1 sa0 sa1 sa2").split():
+    ARENA["float32"][_n] = 192
+for _n in "stx z p2 ev".split():
+    ARENA["float32"][_n] = 256
+for _n, _w in (("k2", 96), ("k3", 48)):
+    ARENA["float32"][_n] = _w
+for _n in "k4 lb lb13 lb8 bar32 thr xkf sxf posf kxd kxd0 bx wf sd1 fnd pge uo rc".split():
+    ARENA["float32"][_n] = 16
+for _n in "asi asj aqi aqj ci cj".split():
+    ARENA["int32"][_n] = 192
+for _n in "vi m7 eni".split():
+    ARENA["int32"][_n] = 256
+ARENA["int32"]["p5r"] = 64
+for _n in "pi bi kxi xk sxi di d1 sdi pr kb cb ui uj ri rj1".split():
+    ARENA["int32"][_n] = 16
+for _n, _w in (("sxu", 16), ("posu", 16), ("uu", 16), ("cu", 192), ("SU0", 192)):
+    ARENA["uint16"][_n] = _w
+for _t in (1, 2, 3):
+    for _n, _w, _d in (("SU", 192, "uint16"), ("QU", 192, "uint16"), ("SL", 256, "bfloat16")):
+        BUFS[_d]["%s%d" % (_n, _t)] = _w
+        BUFS[_d]["o%s%d" % (_n, _t)] = _w
+SCRATCH, WID, PLACE = {}, {}, {}
+for _d in BUFS:
+    for _n in BUFS[_d]:
+        WID[_n] = BUFS[_d][_n]
+        PLACE[_n] = (_n, 0, WID[_n])
+    _a, _o = "ar_" + _d, 0
+    for _n in ARENA[_d]:
+        PLACE[_n] = (_a, _o, ARENA[_d][_n])
+        _o += ARENA[_d][_n]
+    WID[_a] = _o
+    for _n in list(BUFS[_d]) + [_a]:
+        SCRATCH[_n] = ("sbuf", [128, WID[_n]], _d)
+PS = ["P%d" % i for i in range(8)]
+for _n in PS:
+    WID[_n] = 512
+    PLACE[_n] = (_n, 0, 512)
+    SCRATCH[_n] = ("psum", [128, 512], "float32")
+MSG = ["SL", "SU", "QU"]
+LOADS = ["actl", "whyl", "barl", "stl", "PT", "E0", "E1", "E2", "E3"]
+SEMAPHORES = ["sv", "sa", "st", "sg", "loc", "rel"] + ["ld" + n for n in LOADS] + ["out0", "out1", "out2"] \
+    + ["a%s%d" % (n, t) for n in MSG for t in (1, 2, 3)] + ["h%s%d" % (n, t) for n in MSG for t in (1, 2, 3)]
+
+CFG = {"xdve": [0, 0, 0, 0], "fa": [1, 4, 7, 10], "cs": [], "cq": list(range(1, 12)), "wake": 0.1, "eps": 0.05}
+PLAN = {}
+
+
+def route(T, topo, p, kind):
+    src = T.cores[p]
+    dst = T.cores[(p + (STATE_STEP if kind == "SL" else PLAN_STEP)) % N]
+    if topo.may_write(src, dst):
+        return src, dst, None
+    hs = [h for h in topo.cores_of(src) if h != src and topo.may_write(h, dst)]
+    hs.sort(key=lambda h: topo.die(h) != topo.die(src))
+    return src, dst, hs[0 if kind == "SU" else (1 if kind == "SL" else 2 % len(hs))]
+
+
+def send(g, T, topo, src, dst, out, inp, rsem, lsem):
+    rid, pid = topo.addr(dst, src)
+    m = topo.mask(src, dst)
+    g.remote_dma(out_ap=out, in_ap=inp, remote_sem=T.sem[rsem], local_sem=T.sem[lsem], pid=pid, routing_id=rid, dma_engine_mask=m)
+    return len(topo.engines(src, dst))
+
+
+def helper_program(g, core, T, topo):
+    jobs = []
+    for t in (1, 2, 3):
+        for kind in MSG:
+            for p in range(N):
+                src, dst, h = route(T, topo, p, kind)
+                if h == core:
+                    jobs.append((t, kind, src, dst))
+    n = 0
+    for t, kind, src, dst in jobs:
+        g.wait_ge(T.sem["h%s%d" % (kind, t)], len(topo.engines(src, core)))
+        b = "%s%d" % (kind, t)
+        n += send(g, T, topo, core, dst, T[b][:], T["o" + b][:], "a" + b, "rel")
+    if n:
+        g.wait_ge(T.sem["rel"], n)
+
+
+def rank_program(g, core, T, topo):
+    rank = T.rank_of(core)
+    if rank is None:
+        helper_program(g, core, T, topo)
+        return
+    eng = {"sv": g.vector, "sa": g.scalar, "st": g.tensor, "sg": g, "sync": g.sync}
+    banks = set(PS)
+    ops = []
+    hist = {}
+
+    def meet(a, b):
+        if a[1] >= b[2] or b[1] >= a[2]: return False
+        return a[3] != b[3] or a[3] == 1 or (a[1] - b[1]) % a[3] == 0
+
+    def emit(q, fns, reads, writes, cost=0.08, sem=None, inc=1, lat=0.0, after=()):
+        n, pred = len(ops), set(after)
+        for vs, wrt in ((reads, False), (writes, True)):
+            for v in vs:
+                bank = v[0] in banks
+                h = hist.setdefault(v[0] if bank else v[4], [])
+                for i, u, w in h:
+                    if (bank and ops[i][0] != q) or ((w or wrt) and meet(u, v)): pred.add(i)
+                if wrt and v[3] == 1:
+                    h[:] = [e for e in h if not (v[1] <= e[1][1] and e[1][2] <= v[2] and (not bank or ops[e[0]][0] == q))]
+        ops.append([q, fns if isinstance(fns, list) else [fns], pred, cost, sem or q, inc, lat])
+        for vs, wrt in ((reads, False), (writes, True)):
+            for v in vs:
+                hist[v[0] if v[0] in banks else v[4]].append((n, v, wrt))
+        return n
+
+    def schedule():
+        n = len(ops)
+        succ = [[] for _ in range(n)]
+        for i, o in enumerate(ops):
+            for p in o[2]: succ[p].append(i)
+        prio = [0.0] * n
+        for i in range(n - 1, -1, -1):
+            o = ops[i]
+            prio[i] = o[3] + o[6] + max([prio[j] + CFG["wake"] for j in succ[i]] + [0.0])
+        left = [len(o[2]) for o in ops]
+        ready = [0.0] * n
+        free = {}
+        pool = {}
+        order = []
+        for i in range(n):
+            if not left[i]: pool.setdefault(ops[i][0], []).append(i)
+        while len(order) < n:
+            best = None
+            for q in pool:
+                if not pool[q]: continue
+                f = free.get(q, 0.0)
+                lo = min(max(f, ready[i]) for i in pool[q])
+                i = max((j for j in pool[q] if max(f, ready[j]) <= lo + CFG["eps"]), key=lambda j: (prio[j], -j))
+                st = max(f, ready[i])
+                if best is None or st < best[0]: best = (st, i, q)
+            st, i, q = best
+            pool[q].remove(i)
+            order.append(i)
+            o = ops[i]
+            if q != "arr": free[q] = st + o[3]
+            for j in succ[i]:
+                ready[j] = max(ready[j], st + o[3] + o[6] + CFG["wake"])
+                left[j] -= 1
+                if not left[j]: pool.setdefault(ops[j][0], []).append(j)
+        return order
+
+    def issue(order):
+        cnt, tok, snap = {}, {}, {}
+        known = {q: {} for q in eng}
+        for i in order:
+            q, fns, pred, _c, s, inc, _l = ops[i]
+            if q == "arr":
+                tok[i] = (s, inc)
+                cnt[s] = inc
+                continue
+            k = known[q]
+            w = {}
+            for p in pred:
+                if q == "st" and ops[p][0] == "st": continue
+                if tok[p]: w[tok[p][0]] = max(w.get(tok[p][0], 0), tok[p][1])
+            for z in sorted(w):
+                for y in w:
+                    if y != z and snap.get((y, w[y]), {}).get(z, 0) >= w[z] and k.get(z, 0) < w[z] and k.get(y, 0) < w[y]:
+                        break
+                else:
+                    if k.get(z, 0) < w[z]: eng[q].wait_ge(T.sem[z], w[z])
+            for z in w:
+                k[z] = max(k.get(z, 0), w[z])
+                for s2, c2 in snap.get((z, w[z]), {}).items():
+                    if k.get(s2, 0) < c2: k[s2] = c2
+            for f in fns[:-1]: f(eng[q])
+            r = fns[-1](eng[q])
+            tok[i] = None
+            if s != "none":
+                r.then_inc(T.sem[s], inc)
+                cnt[s] = cnt.get(s, 0) + inc
+                tok[i] = (s, cnt[s])
+                snap[tok[i]] = dict(k)
+        for z in sorted(cnt):
+            if known["sg"].get(z, 0) < cnt[z]: g.wait_ge(T.sem[z], cnt[z])
+
+    def V(n, lo=0, hi=None, step=1):
+        b, o, w = PLACE[n]
+        return (b, o + lo, o + (w if hi is None else hi), step, n)
+
+    def IND(win, off):
+        return ("ind", win, off)
+
+    def ap(v):
+        if len(v) == 3: return T[v[1]][:, 0:WID[v[1]]].indirect(ap(v[2]))
+        return T[v[0]][:, v[1]:v[2]:v[3]] if v[3] != 1 else T[v[0]][:, v[1]:v[2]]
+
+    def rl(*vs):
+        o = []
+        for v in vs:
+            if isinstance(v, tuple):
+                o += [V(v[1]), v[2]] if len(v) == 3 else [v]
+        return o
+
+    def sc(x):
+        return ap(x) if isinstance(x, tuple) else x
+
+    def el(v):
+        return 16 * el(v[2]) if len(v) == 3 else -(-(v[2] - v[1]) // v[3])
+
+    CY = 0.00083 * 1.2
+
+    def price(out, ins, per, ind=0.05):
+        if len(out) == 3: return ind + el(out) * 3.5 * CY
+        if any(len(i) == 3 for i in ins): return ind + el(out) * 1.5 * CY
+        return max(64, el(out) * per) * CY
+
+    def two(*vs):
+        return all(len(v) == 5 and v[0] not in banks and SCRATCH[v[0]][2] in ("bfloat16", "uint16") for v in vs)
+
+    def ts(out, i0, s1, op0, s2=None, op1=None):
+        if op1 is None: f = lambda e: e.tensor_scalar(ap(out), ap(i0), sc(s1), None, op0)
+        else: f = lambda e: e.tensor_scalar(ap(out), ap(i0), sc(s1), sc(s2), op0, op1)
+        emit("sv", f, rl(i0, s1, s2), [out], price(out, [i0], 0.5 if two(out, i0) else 1))
+
+    def tt(out, i0, i1, op):
+        f = lambda e: e.tensor_tensor(ap(out), ap(i0), ap(i1), op)
+        c = price(out, [i0], 1 if i0[0] in banks or i1[0] in banks else 2)
+        if len(out) == 3: emit("sv", f, rl(i0, i1, out[2]), [V(out[1])], c)
+        else: emit("sv", f, rl(i0, i1), [out], c)
+
+    def cp(out, i0):
+        f = lambda e: e.tensor_copy(ap(out), ap(i0))
+        c = price(out, [i0], 0.5 if two(out, i0) else 1)
+        if len(out) == 3: emit("sv", f, rl(i0, out[2]), [V(out[1])], c)
+        else: emit("sv", f, rl(i0), [out], c)
+
+    def ms(out, c):
+        emit("sv", lambda e: e.memset(ap(out), c), [], [out], price(out, [], 0.5 if two(out) else 1))
+
+    def act(out, i0, func=F.Identity, scale=1.0, bias=0.0, acc=None):
+        if acc is None: f = lambda e: e.activation(ap(out), ap(i0), func, bias=bias, scale=scale)
+        else: f = lambda e: e.activation(ap(out), ap(i0), func, bias=bias, scale=scale, accum_out=ap(acc))
+        emit("sa", f, rl(i0), [out] + ([acc] if acc else []), price(out, [i0], 1, 0.065))
+
+    def mms(*jobs):
+        fs = [lambda e, j=j: e.matmul(ap(j[0]), ap(j[1]), ap(j[2]), j[3], j[4]) for j in jobs]
+        emit("st", fs, [v for j in jobs for v in (j[1], j[2])], [j[0] for j in jobs], sum(max(64, el(j[2])) for j in jobs) * CY)
+
+    def load(q, sem, out, src):
+        emit(q, lambda e: e.dma_start(ap(out), src), [], [out], sem="ld" + sem, inc=16, lat=2.5)
+
+    def store(sem, dst, src):
+        emit("sync", lambda e: e.dma_start(dst, ap(src)), [src], [], sem=sem, inc=16, lat=2.5)
+
+    def rowsum(out, selb, buf, lo, hi, step, before=()):
+        mms(*(list(before) + [(out, V(selb, 128 * j, 128 * j + 128), V(buf, lo + j * step, hi, 16 * step),
+                               not before and j == 0, j == 15) for j in range(16)]))
+
+    def rep(bank, lo, src):
+        mms(*[(V(bank, lo + 16 * k, lo + 16 * k + 16), V("idn"), V(src), True, True) for k in range(L)])
+
+    def tree(src, out, other=None):
+        tt(V("k2"), V(src, 0, 96), V(src, 96, 192), A.max)
+        tt(V("k3"), V("k2", 0, 48), V("k2", 48, 96), A.max)
+        tt(V("k4"), V("k3", 0, 16), V("k3", 16, 32), A.max)
+        last = V("k3", 32, 48)
+        if other:
+            tt(V("wf"), last, other, A.max)
+            last = V("wf")
+        tt(out, V("k4"), last, A.max)
+
+    def compact(z, acc, scalar):
+        ts(V(acc), V(z), 0.0, A.max, 4096.0, A.min)
+        ws = [192 - 16 * r for r in range(L)]
+        spot = lambda r: V("P%d" % (3 + r % 2) if r in scalar else "P7", 192 * (r % 2), 192 * (r % 2) + ws[r])
+        rs = sorted(range(1, L), key=lambda r: (r in scalar, r))
+        for i in range(L):
+            if i < L - 1:
+                r = rs[i]
+                if r in scalar:
+                    sa = V("sa%d" % (r % 3), 0, ws[r])
+                    act(sa, V(z, 16 * r, 192), F.Relu, bias=-4096.0 * r)
+                    act(spot(r), sa, F.Relu, scale=-1.0, bias=4096.0)
+                else: ts(spot(r), V(z, 16 * r, 192), 4096.0 * r, A.max, 4096.0 * (r + 1), A.min)
+            if i:
+                r = rs[i - 1]
+                tt(V(acc, 0, ws[r]), V(acc, 0, ws[r]), spot(r), A.subtract if r in scalar else A.add)
+
+    blk = lambda n, k, w=16: V(n, w * k, w * k + w)
+    SP = lambda sh=0: V("P6", 16 - sh, 208 - sh)
+    QP = lambda sh=0: V("P6", 224 - sh, 416 - sh)
+    TA, TB, TC = V("P7", 0, 192), V("P7", 192, 384), V("P5", 256, 512)
+    TD = V("P7", 384, 448)
+    Z = V("P2", 256, 448)
+
+    load("sync", "E0", V("E", 0, 512), T.eff[:, 0:512])
+    load("sa", "actl", V("actl"), T.act[:, :])
+    load("sync", "E1", V("E", 512, 1024), T.eff[:, 512:1024])
+    load("sa", "stl", V("stl"), T.st0[:, :])
+    load("sync", "E2", V("E", 1024, 1536), T.eff[:, 1024:1536])
+    load("sa", "PT", V("PT"), T.req[:, :])
+    load("sync", "E3", V("E", 1536, 2048), T.eff[:, 1536:2048])
+    load("sync", "whyl", V("whyl"), T.why[:, :])
+    load("sync", "barl", V("barl"), T.bar[:, :])
+    ms(V("ones"), 1.0)
+
+    def aff(out, src, pattern, op, base, cm):
+        emit("sg", lambda e: e.affine_select(ap(V(out)), ap(V(src)), pattern, op, 0.0, base, cm), [V(src)], [V(out)], 0.4)
+    aff("idn", "ones", [[-1, 128]], A.is_equal, 0, 1)
+    aff("bd1", "ones", [[-16, 8], [0, 16]], A.is_ge, 0, 1)
+    aff("bd", "bd1", [[16, 8], [0, 16]], A.is_ge, 15, -1)
+    emit("sg", lambda e: e.iota(ap(V("pi")), [[0, 16]], 0, 1), [], [V("pi")])
+    emit("sg", lambda e: e.iota(ap(V("bi")), [[16, 16]], 0, 0), [], [V("bi")])
+    emit("sg", lambda e: e.iota(ap(V("ki")), [[-1, 12], [0, 16]], 12, 0, allow_small_or_imprecise_dtypes=True), [], [V("ki")])
+    ms(V("sel"), 0.0)
+    ms(V("c512"), 512.0)
+    ms(V("cm15"), -1536.0)
+    ms(V("P6", 0, 16), 0.0)
+    ms(V("P6", 208, 224), 0.0)
+    ms(V("thr"), THR0 + 1024.0)
+    ms(V("NB", 0, NX, 13), 0.0)
+    ts(V("i4k"), V("idn"), 4096.0, A.mult)
+    ts(V("i64k"), V("idn"), 65536.0, A.mult)
+    ts(V("i249"), V("idn"), 249.0, A.mult)
+    cp(V("SU0"), V("actl"))
+    ts(V("c0t"), V("stl"), 8.0, A.is_lt, 104.0, A.mult)
+    ts(V("c8t"), V("stl"), -8.0, A.add)
+    for c in range(4):
+        sl = (512 * c, 512 * c + 512)
+        P = V(PS[2 + c])
+        ts(V("t120", *sl), V("E", *sl), 12.0, A.is_lt, 120.0, A.mult)
+        act(V("e8", *sl), V("E", *sl), bias=-8.0)
+        act(V("qa", *sl), V("E", *sl), F.Abs, bias=-7.5)
+        mms((P, V("idn"), V("e8", *sl), True, False), (P, V("idn"), V("t120", *sl), False, True))
+        ts(V("mm", *sl), V("qa", *sl), 4.0, A.is_ge)
+        tt(V("X8", *sl), V("mm", *sl), P, A.mult)
+
+    def late_setup():
+        ts(V("nb0"), V("PT"), 12.0, A.is_ge)
+        ts(V("ND"), V("nb0"), NDO, A.mult, ND0, A.add)
+        tt(V("Gb", 0, NX, 13), V("c0t"), V("c8t"), A.add)
+        ts(V("SF"), V("actl"), 1.0, A.add)
+        ts(SP(), V("actl"), 1.0, A.add)
+        ts(V("QF"), V("whyl"), 1.0, A.add)
+        ts(QP(), V("whyl"), 1.0, A.add)
+        ts(V("ckx"), V("ki"), 2048.0, A.mult, -1.0, A.add)
+        ts(V("ckd"), V("ki"), -2048.0, A.mult, 26624.0 + 65535.0, A.add)
+        ts(V("ckm"), V("ki"), 2048.0, A.mult, -2048.0, A.add)
+        ts(V("pi"), V("pi"), 15, A.bitwise_and)
+        tt(V("lb"), V("pi"), V("bi"), A.add)
+        ts(V("lb13"), V("lb"), 13.0, A.mult, 12.0, A.add)
+        ts(V("lb8"), V("lb"), 8.0, A.mult)
+        for j in range(16):
+            cp(V("sel", 129 * j, 128 * j + 128, 16), V("bd", j, 128, 16))
+        ts(V("sels"), V("sel"), 2048.0, A.mult)
+        ts(V("bar32"), V("barl"), 32768.0, A.mult)
+
+    nloc = [0]
+
+    def post(kind, t):
+        b = "%s%d" % (kind, t)
+        src, dst, h = route(T, topo, rank, kind)
+
+        def go(e):
+            if h is None: nloc[0] += send(g, T, topo, src, dst, T[b][:], T["o" + b][:], "a" + b, "loc")
+            else: nloc[0] += send(g, T, topo, src, h, T["o" + b][:], T["o" + b][:], "h" + b, "loc")
+        n = emit("sg", go, [V("o" + b)], [], 0.4, sem="none", lat=2.5)
+        p2 = (rank - (STATE_STEP if kind == "SL" else PLAN_STEP)) % N
+        s2, d2, h2 = route(T, topo, p2, kind)
+        emit("arr", [], [], [V(b)], 0.0, sem="a" + b, inc=len(topo.engines(s2 if h2 is None else h2, core)), after=(n,))
+
+    for t in range(VI):
+        last = t == VI - 1
+        su = "SU%d" % t
+        off = lambda k: V(su, 16 * k, 16 * k + 16)
+        fa = CFG["fa"]
+        xd = range(L - CFG["xdve"][t], L)
+        for k in range(L):
+            if k not in xd: act(V("Gb", 1 + k, NX, 13), IND("X8", off(k)), bias=-8.0)
+        if t:
+            cp(V("Gb", 0, NX, 13), V("SL%d" % t))
+            ts(V("SF"), V(su), 1.0, A.add)
+            ts(SP(), V(su), 1.0, A.add)
+        else:
+            late_setup()
+        tt(V("KX"), V("ckx"), SP(), A.add)
+        tt(V("KD"), V("ckd"), SP(), A.add)
+        for k in xd: ts(V("Gb", 1 + k, NX, 13), IND("X8", off(k)), -8.0, A.add)
+        for k in range(L):
+            ts(V("NB", 1 + k, NX, 13), V("Gb", 1 + k, NX, 13), -4.5, A.is_lt)
+        for k in fa: act(blk("ng", k, 256), IND("nb0", off(k)), F.Copy)
+        emit("sv", lambda e: e.tensor_tensor_scan(ap(V("ST")), ap(V("NB")), ap(V("Gb")), 0.0, A.mult, A.add), [V("NB"), V("Gb")], [V("ST")], NX / 2 * CY)
+        for k in range(L):
+            if k in fa:
+                j = fa.index(k)
+                P = V(PS[3 + j % 3], 256 * (j // 3), 256 * (j // 3) + 256)
+                mms((P, V("i249"), blk("ng", k, 256), True, False), (P, V("idn"), V("ST", k, NX, 13), False, True))
+                act(blk("Yb", k, 256), P, bias=ND0 - 0.5)
+            else:
+                tt(blk("Yb", k, 256), IND("ND", off(k)), V("ST", k, NX, 13), A.add)
+        for q in range(3): rowsum(blk("P0", q, 64), "sel", "Yb", 1024 * q, 1024 * q + 1024, 1)
+        rowsum(V("P2", 128, 144), "sel", "ST", 12, NX, 13)
+        cp(V("vi"), V("ST", 12, NX, 13))
+        ts(V("m7"), V("vi"), 7, A.bitwise_and)
+        if not last:
+            ts(TC, V("ST", 12, NX, 13), 0.0, A.is_ge, 96.0, A.mult)
+            tt(V("oSL%d" % (t + 1)), V("m7"), TC, A.add)
+            post("SL", t + 1)
+        ts(TA, V("P0", 0, 192), V("thr", 0, 1), A.is_ge)
+        tt(V("kk"), V("KX"), TA, A.mult)
+        tree("kk", V("kxi"))
+        ts(V("xk"), V("kxi"), 11, A.logical_shift_right)
+        ts(V("sxi"), V("kxi"), 2047, A.bitwise_and)
+        tt(V("posf"), V("lb13"), V("xk"), A.subtract)
+        cp(V("sxu"), V("sxi"))
+        cp(V("posu"), V("posf"))
+        cp(V("sxf"), V("sxi"))
+        ts(V("stx"), IND("ST", V("posu")), KZ, A.add)
+        cp(V("xkf"), V("xk"))
+        cp(V("xkb"), V("xk"))
+        tt(V("z"), IND("ND", V("sxu")), V("stx"), A.add)
+        for m in range(6): act(blk("am", m), V("sxf"), scale=float(KAP[m]), bias=float(97 * t))
+        act(V("bx"), V("xkf"), F.Exp, scale=-LNB, bias=11 * LNB)
+        act(V("wx"), V("z"), F.Exp, scale=LNB / 8, bias=LNB / 8 * (-104.0 - (ND0 + NDO + KZ)))
+        for m in range(6, L): act(blk("am", m), V("sxf"), scale=float(KAP[m]), bias=float(97 * t))
+        rep("P0", 192, "xkb")
+        rowsum(V("P2", 0, 16), "sel", "wx", 0, 256, 1)
+        ts(TC, V("z"), -3064.5, A.max, -3060.5, A.min)
+        ts(V("p2"), V("z"), ND0 + 256.0 + KZ, A.is_ge, 8.0, A.mult)
+        tt(V("P3", 0, 256), V("p2"), TC, A.subtract)
+        ts(V("kxd0"), V("xkf"), -2048.0, A.mult, 26624.0, A.add)
+        tt(V("kxd"), V("kxd0"), V("sxf"), A.add)
+        tt(V("eqm"), V("ki"), V("P0", 192, 384), A.is_equal)
+        tt(V("gt"), V("ki"), V("P0", 192, 384), A.is_lt)
+        tt(V("wf"), V("bx"), V("P2", 0, 16), A.mult)
+        for k in range(L):
+            lim = float(0.5 * 512.0 ** k)
+            if k < 7: ts(V("P7", 192 + 16 * k, 208 + 16 * k), V("wf"), lim, A.is_ge)
+            else: act(V("P3", 256 + 16 * k, 272 + 16 * k), V("wf"), F.Sign, bias=-lim)
+        tt(V("dk0", 0, 112), V("KD", 0, 112), V("P7", 192, 304), A.mult)
+        tt(V("dk0", 112, 192), V("KD", 112, 192), V("P3", 368, 448), A.mult)
+        tree("dk0", V("di"), V("kxd"))
+        ts(V("sdi"), V("di"), 2047, A.bitwise_and)
+        tt(V("pr"), V("sxf"), V("sdi"), A.mult)
+        ts(V("d1"), V("di"), 11, A.logical_shift_right, 15, A.bitwise_and)
+        for j in range(4): ts(blk("p5r", j), V("pr"), 5, A.logical_shift_right)
+        ts(V("sd1"), V("sdi"), 1.0, A.add)
+        for h in range(3):
+            tt(blk("ci", h, 64), blk("am", h, 64), V("p5r"), A.add)
+            if h == 0: ts(V("dkb"), V("d1"), -1.0, A.mult, 13.0, A.add)
+            ts(blk("cj", h, 64), blk("ci", h, 64), 2047, A.bitwise_and)
+            cp(blk("cu", h, 64), blk("cj", h, 64))
+        rep("P1", 192, "dkb")
+        for m in range(L):
+            if m == 2:
+                for k in range(L): act(blk("P5", k), V("sd1"))
+            act(blk("eg", m, 256), IND("E", blk("cu", m)), F.Copy)
+
+        def cadd(h):
+            for m in range(4 * h, 4 * h + 4):
+                tt(blk("yc", m, 256), blk("eg", m, 256), V("P3", 0, 256), A.add)
+            o = blk("P4", h, 64)
+            rowsum(o, "sels", "yc", 1024 * h, 1024 * h + 1024, 1, [(o, V("c512"), V("cm15"), True, False)])
+
+        tt(V("gem"), V("gt"), V("eqm"), A.add)
+        tt(V("dr0"), V("gt"), SP(16), A.mult)
+        tt(TA, V("gem"), SP(), A.mult)
+        tt(V("dis"), V("dr0"), TA, A.subtract)
+        ts(V("fnd"), V("xkf"), 1.0, A.is_ge)
+        if t:
+            cp(V("QF"), V("QU%d" % t))
+            cp(QP(), V("QU%d" % t))
+        tt(V("goq"), V("QF"), V("P5", 0, 192), A.is_equal)
+        tt(TB, V("ki"), V("P1", 192, 384), A.is_equal)
+        tt(V("go"), V("goq"), TB, A.max)
+        mms(*([(Z, V("i64k"), V("go"), True, False)] + [
+            (V("P2", 256 + 16 * s, 448), V("i4k"), V("go", 0, 192 - 16 * s), False, s == L - 1) for s in range(1, L)]))
+        cadd(0)
+        ts(V("c1"), V("cj"), 1.0, A.add)
+        tt(V("kadd"), V("cj"), V("ckm"), A.add)
+        tt(V("zs"), V("SF"), Z, A.add)
+        cadd(1)
+        compact("zs", "asi", CFG["cs"])
+        cadd(2)
+        ts(V("asj"), V("asi"), 4095, A.bitwise_and)
+        ts(TA, V("asj"), 0.0, A.is_equal)
+        tt(TA, V("c1"), TA, A.mult)
+        tt(V("dr0"), V("asj"), TA, A.add)
+        tt(V("dr"), V("dr0"), SP(), A.subtract)
+        cp(V("ui"), V("P2", 128, 144))
+        ts(V("uj"), V("ui"), 7, A.bitwise_and)
+        tt(V("uo"), V("lb8"), V("uj"), A.add)
+        ts(TC, V("ST", 12, NX, 13), 0.0, A.is_lt, 8.0, A.mult)
+        cp(V("uu"), V("uo"))
+        tt(V("sfin"), V("m7"), TC, A.add)
+        tt(V("ev"), IND("E", V("uu")), V("sfin"), A.add)
+        ts(V("enb"), V("ev"), 0.5, A.mult, 159.75, A.add)
+        act(V("en"), V("enb"), bias=-160.0)
+        if not last:
+            act(V("u8"), V("enb"), bias=-168.0)
+            act(V("uq"), V("enb"), F.Abs, bias=-167.5)
+        tt(V("kk"), V("kadd"), V("P4", 0, 192), A.add)
+        tree("kk", V("kb"))
+        tt(V("pge"), V("kb"), V("bar32"), A.is_ge)
+        ts(V("cb"), V("kb"), 2047, A.bitwise_and)
+        tt(V("put"), V("pge"), V("fnd"), A.mult)
+        for j in range(4): ts(V("P7", 384 + 16 * j, 400 + 16 * j), V("cb"), 1.0, A.add)
+        tt(V("ret"), V("fnd"), V("put"), A.subtract)
+        rep("P0", 0, "put")
+        rep("P1", 0, "ret")
+        for j in range(3): tt(V("P7", 64 * j, 64 * j + 64), blk("eqm", j, 64), TD, A.mult)
+        tt(V("na"), V("dis"), TA, A.add)
+        tt(TB, V("dr"), V("P1", 0, 192), A.mult)
+        tt(V("nc"), V("SF"), TB, A.add)
+        tt(TA, V("na"), V("P0", 0, 192), A.mult)
+        tt(V("na"), V("nc"), TA, A.add)
+        if not last:
+            ts(V("oSU%d" % (t + 1)), V("na"), -1.0, A.add)
+            post("SU", t + 1)
+            act(V("rj"), V("ret"), F.Copy, acc=V("rc", 0, 1))
+            act(V("rcb", 0, 1), V("rc", 0, 1), F.Copy)
+            mms((V("P2", 64, 65), V("ones"), V("rcb", 0, 1), True, True))
+            ts(TC, V("enb"), 172.0, A.is_lt, 120.0, A.mult)
+            ts(V("um"), V("uq"), 4.0, A.is_ge)
+            tt(V("uh"), V("u8"), TC, A.add)
+            tt(IND("X8", V("uu")), V("uh"), V("um"), A.mult)
+            cp(IND("E", V("uu")), V("en"))
+        else:
+            ts(V("ysf"), V("na"), -1.0, A.add)
+            store("out0", T.ys[:, :], V("ysf"))
+            cp(IND("E", V("uu")), V("en"))
+            store("out2", T.ye[:, :], V("E"))
+        tt(V("zq"), V("QF"), Z, A.add)
+        compact("zq", "aqi", CFG["cq"])
+        tt(V("drq"), V("gt"), QP(16), A.mult)
+        tt(TA, V("gem"), QP(), A.mult)
+        ts(V("aqj"), V("aqi"), 4095, A.bitwise_and)
+        tt(V("diq"), V("drq"), TA, A.subtract)
+        tt(TA, V("eqm"), V("P5", 0, 192), A.mult)
+        tt(V("drq"), V("aqj"), QP(), A.subtract)
+        tt(V("qa1"), V("diq"), TA, A.add)
+        tt(TA, V("qa1"), V("P0", 0, 192), A.mult)
+        tt(V("qc1"), V("QF"), TA, A.add)
+        tt(TB, V("drq"), V("P1", 0, 192), A.mult)
+        tt(V("qa1"), V("qc1"), TB, A.add)
+        if not last:
+            cp(V("oQU%d" % (t + 1)), V("qa1"))
+            post("QU", t + 1)
+            cp(V("ri", 0, 1), V("P2", 64, 65))
+            ts(V("rj1", 0, 1), V("ri", 0, 1), 1, A.bitwise_and)
+            ts(V("thr", 0, 1), V("rj1", 0, 1), 512.0, A.mult, THR0 + 1024.0, A.add)
+        else:
+            ts(V("ywf"), V("qa1"), -1.0, A.add)
+            store("out1", T.yw[:, :], V("ywf"))
+    if "order" not in PLAN: PLAN["order"] = schedule()
+    issue(PLAN["order"])
+    g.wait_ge(T.sem["loc"], nloc[0])

@@ -17,24 +17,26 @@ for _n in "E X8 PT t120 e8 qa mm nb0 sel sels".split():
     BUFS["bfloat16"][_n] = W
 for _n in "Gb NB ST".split():
     BUFS["bfloat16"][_n] = NX
-for _n in "Yb eg yc ng".split():
+for _n in "Yb egb yc ng".split():
     BUFS["bfloat16"][_n] = 3072
-for _n in "ones idn bd1 bd i4k i64k i249 c512".split():
+MULT = [("i4k", 4096.0), ("i64k", 65536.0), ("i249", 249.0), ("im1", -1.0), ("i48", 48.0), ("im4", -4.0), ("im2", -2.0), ("i4", 4.0), ("im60", -60.0)]
+for _n in "ones idn bd1 bd c512".split() + [_m[0] for _m in MULT]:
     BUFS["bfloat16"][_n] = 128
 BUFS["float32"]["ND"] = W
+BUFS["float32"]["eg"] = 3072
 for _n, _w in (("actl", 192), ("whyl", 192), ("barl", 16)):
     BUFS["int32"][_n] = _w
 BUFS["bfloat16"]["stl"] = 256
 BUFS["float32"]["ysf"] = BUFS["float32"]["ywf"] = 192
-for _n in "c0t c8t wx sfin enb en u8 uq um uh".split():
+for _n in "c0t c8t wx sfin enb en uq um uh rnd sg sn sf".split():
     ARENA["bfloat16"][_n] = 256
-for _n, _w in (("cm15", 64), ("go", 192), ("xkb", 16), ("dkb", 16), ("put", 16), ("ret", 16), ("rj", 16), ("rcb", 16)):
+for _n, _w in (("cm15", 64), ("ckm", 192), ("go", 192), ("xkb", 16), ("dkb", 16), ("shb", 16), ("slb", 16), ("put", 16), ("ret", 16), ("rj", 16), ("rcb", 16)):
     ARENA["bfloat16"][_n] = _w
 for _n in "SF QF".split():
     ARENA["float32"][_n] = 192
-for _n in ("ki ckx ckd ckm KX KD kk am dk0 kadd goq zs zq tlc dr dr0 drq dis diq eqm gt gem c1 na nc qa1 qc1 sa0 sa1 sa2").split():
+for _n in ("ki ckx ckd KX KD kk am dk0 goq zs zq tlc dr dr0 drq dis diq eqm gt gem c1 na nc qa1 qc1 sa0 sa1 sa2").split():
     ARENA["float32"][_n] = 192
-for _n in "stx z p2 ev".split():
+for _n in "stx z ev".split():
     ARENA["float32"][_n] = 256
 for _n, _w in (("k2", 96), ("k3", 48)):
     ARENA["float32"][_n] = _w
@@ -42,10 +44,8 @@ for _n in "k4 lb lb13 lb8 bar32 thr xkf sxf posf kxd kxd0 bx wf sd1 fnd pge uo r
     ARENA["float32"][_n] = 16
 for _n in "asi asj aqi aqj ci cj".split():
     ARENA["int32"][_n] = 192
-for _n in "vi m7 eni".split():
-    ARENA["int32"][_n] = 256
 ARENA["int32"]["p5r"] = 64
-for _n in "pi bi kxi xk sxi di d1 sdi pr kb cb ui uj ri rj1".split():
+for _n in "pi bi kxi xk sxi di d1 sdi sh sl pr kb cb ui uj ri rj1".split():
     ARENA["int32"][_n] = 16
 for _n, _w in (("sxu", 16), ("posu", 16), ("uu", 16), ("cu", 192), ("SU0", 192)):
     ARENA["uint16"][_n] = _w
@@ -75,25 +75,32 @@ LOADS = ["actl", "whyl", "barl", "stl", "PT", "E0", "E1", "E2", "E3"]
 SEMAPHORES = ["sv", "sa", "st", "sg", "loc", "rel"] + ["ld" + n for n in LOADS] + ["out0", "out1", "out2"] \
     + ["a%s%d" % (n, t) for n in MSG for t in (1, 2, 3)] + ["h%s%d" % (n, t) for n in MSG for t in (1, 2, 3)]
 
-CFG = {"xdve": [0, 0, 0, 0], "fa": [1, 4, 7, 10], "cs": [], "cq": list(range(1, 12)), "wake": 0.1, "eps": 0.05}
+CFG = {"xdve": [2, 4, 4, 4], "fa": [1, 4, 7, 10], "ca": [], "cs": list(range(4, 12)), "sd": 2, "late": {"SL": 10.0, "SU": 0.5, "QU": 5.0}, "cq": list(range(1, 12)), "wake": 0.15, "eps": 0.05}
 PLAN = {}
 
 
 def route(T, topo, p, kind):
     src = T.cores[p]
     dst = T.cores[(p + (STATE_STEP if kind == "SL" else PLAN_STEP)) % N]
-    if topo.may_write(src, dst):
+    plan = T.cores[(p + PLAN_STEP) % N]
+    if topo.may_write(src, dst) and topo.may_write(src, plan):
         return src, dst, None
-    hs = [h for h in topo.cores_of(src) if h != src and topo.may_write(h, dst)]
+    if topo.may_write(src, dst) and kind != "SL":
+        return src, dst, None
+    hs = [h for h in topo.cores_of(src) if h != src and topo.may_write(h, dst) and topo.may_write(h, plan)]
     hs.sort(key=lambda h: topo.die(h) != topo.die(src))
-    return src, dst, hs[0 if kind == "SU" else (1 if kind == "SL" else 2 % len(hs))]
+    return src, dst, hs[0]
 
 
-def send(g, T, topo, src, dst, out, inp, rsem, lsem):
+def send(g, T, topo, src, dst, out, inp, rsem, lsem, final):
     rid, pid = topo.addr(dst, src)
-    m = topo.mask(src, dst)
+    m = topo.mask(src, dst) & topo.mask(dst if dst != final else src, final)
     g.remote_dma(out_ap=out, in_ap=inp, remote_sem=T.sem[rsem], local_sem=T.sem[lsem], pid=pid, routing_id=rid, dma_engine_mask=m)
-    return len(topo.engines(src, dst))
+    return count(topo, src, dst, final)
+
+
+def count(topo, src, dst, final):
+    return len([e for e in topo.engines(src, dst) if e in topo.engines(dst if dst != final else src, final)])
 
 
 def helper_program(g, core, T, topo):
@@ -106,9 +113,9 @@ def helper_program(g, core, T, topo):
                     jobs.append((t, kind, src, dst))
     n = 0
     for t, kind, src, dst in jobs:
-        g.wait_ge(T.sem["h%s%d" % (kind, t)], len(topo.engines(src, core)))
+        g.wait_ge(T.sem["h%s%d" % (kind, t)], count(topo, src, core, dst))
         b = "%s%d" % (kind, t)
-        n += send(g, T, topo, core, dst, T[b][:], T["o" + b][:], "a" + b, "rel")
+        n += send(g, T, topo, core, dst, T[b][:], T["o" + b][:], "a" + b, "rel", dst)
     if n:
         g.wait_ge(T.sem["rel"], n)
 
@@ -275,7 +282,7 @@ def rank_program(g, core, T, topo):
 
     def mms(*jobs):
         fs = [lambda e, j=j: e.matmul(ap(j[0]), ap(j[1]), ap(j[2]), j[3], j[4]) for j in jobs]
-        emit("st", fs, [v for j in jobs for v in (j[1], j[2])], [j[0] for j in jobs], sum(max(64, el(j[2])) for j in jobs) * CY)
+        emit("st", fs, [v for j in jobs for v in (j[1], j[2])], [j[0] for j in jobs], sum(max(64, el(j[2])) * (1 if two(j[2]) else 4) for j in jobs) * CY)
 
     def load(q, sem, out, src):
         emit(q, lambda e: e.dma_start(ap(out), src), [], [out], sem="ld" + sem, inc=16, lat=2.5)
@@ -300,11 +307,14 @@ def rank_program(g, core, T, topo):
             last = V("wf")
         tt(out, V("k4"), last, A.max)
 
-    def compact(z, acc, scalar):
+    def compact(z, acc, scalar, bank):
         ts(V(acc), V(z), 0.0, A.max, 4096.0, A.min)
         ws = [192 - 16 * r for r in range(L)]
-        spot = lambda r: V("P%d" % (3 + r % 2) if r in scalar else "P7", 192 * (r % 2), 192 * (r % 2) + ws[r])
         rs = sorted(range(1, L), key=lambda r: (r in scalar, r))
+
+        def spot(r):
+            i = rs.index(r) % 2
+            return V("P%d" % (bank + i), 0, ws[r]) if r in scalar else V("P7", 192 * i, 192 * i + ws[r])
         for i in range(L):
             if i < L - 1:
                 r = rs[i]
@@ -320,7 +330,8 @@ def rank_program(g, core, T, topo):
     blk = lambda n, k, w=16: V(n, w * k, w * k + w)
     SP = lambda sh=0: V("P6", 16 - sh, 208 - sh)
     QP = lambda sh=0: V("P6", 224 - sh, 416 - sh)
-    TA, TB, TC = V("P7", 0, 192), V("P7", 192, 384), V("P5", 256, 512)
+    TA, TB = V("P7", 0, 192), V("P7", 192, 384)
+    PA, PB = V("P4", 256, 512), V("P5", 256, 512)
     TD = V("P7", 384, 448)
     Z = V("P2", 256, 448)
 
@@ -350,9 +361,7 @@ def rank_program(g, core, T, topo):
     ms(V("P6", 208, 224), 0.0)
     ms(V("thr"), THR0 + 1024.0)
     ms(V("NB", 0, NX, 13), 0.0)
-    ts(V("i4k"), V("idn"), 4096.0, A.mult)
-    ts(V("i64k"), V("idn"), 65536.0, A.mult)
-    ts(V("i249"), V("idn"), 249.0, A.mult)
+    for n, c in MULT[:3]: ts(V(n), V("idn"), c, A.mult)
     cp(V("SU0"), V("actl"))
     ts(V("c0t"), V("stl"), 8.0, A.is_lt, 104.0, A.mult)
     ts(V("c8t"), V("stl"), -8.0, A.add)
@@ -377,6 +386,7 @@ def rank_program(g, core, T, topo):
         ts(V("ckx"), V("ki"), 2048.0, A.mult, -1.0, A.add)
         ts(V("ckd"), V("ki"), -2048.0, A.mult, 26624.0 + 65535.0, A.add)
         ts(V("ckm"), V("ki"), 2048.0, A.mult, -2048.0, A.add)
+        for n, c in MULT[3:]: ts(V(n), V("idn"), c, A.mult)
         ts(V("pi"), V("pi"), 15, A.bitwise_and)
         tt(V("lb"), V("pi"), V("bi"), A.add)
         ts(V("lb13"), V("lb"), 13.0, A.mult, 12.0, A.add)
@@ -393,12 +403,12 @@ def rank_program(g, core, T, topo):
         src, dst, h = route(T, topo, rank, kind)
 
         def go(e):
-            if h is None: nloc[0] += send(g, T, topo, src, dst, T[b][:], T["o" + b][:], "a" + b, "loc")
-            else: nloc[0] += send(g, T, topo, src, h, T["o" + b][:], T["o" + b][:], "h" + b, "loc")
+            if h is None: nloc[0] += send(g, T, topo, src, dst, T[b][:], T["o" + b][:], "a" + b, "loc", dst)
+            else: nloc[0] += send(g, T, topo, src, h, T["o" + b][:], T["o" + b][:], "h" + b, "loc", dst)
         n = emit("sg", go, [V("o" + b)], [], 0.4, sem="none", lat=2.5)
         p2 = (rank - (STATE_STEP if kind == "SL" else PLAN_STEP)) % N
         s2, d2, h2 = route(T, topo, p2, kind)
-        emit("arr", [], [], [V(b)], 0.0, sem="a" + b, inc=len(topo.engines(s2 if h2 is None else h2, core)), after=(n,))
+        emit("arr", [], [], [V(b)], 0.0, sem="a" + b, inc=len(topo.engines(s2 if h2 is None else h2, core)), lat=CFG["late"][kind], after=(n,))
 
     for t in range(VI):
         last = t == VI - 1
@@ -410,8 +420,8 @@ def rank_program(g, core, T, topo):
             if k not in xd: act(V("Gb", 1 + k, NX, 13), IND("X8", off(k)), bias=-8.0)
         if t:
             cp(V("Gb", 0, NX, 13), V("SL%d" % t))
-            ts(V("SF"), V(su), 1.0, A.add)
             ts(SP(), V(su), 1.0, A.add)
+            act(V("SF"), SP())
         else:
             late_setup()
         tt(V("KX"), V("ckx"), SP(), A.add)
@@ -431,12 +441,15 @@ def rank_program(g, core, T, topo):
                 tt(blk("Yb", k, 256), IND("ND", off(k)), V("ST", k, NX, 13), A.add)
         for q in range(3): rowsum(blk("P0", q, 64), "sel", "Yb", 1024 * q, 1024 * q + 1024, 1)
         rowsum(V("P2", 128, 144), "sel", "ST", 12, NX, 13)
-        cp(V("vi"), V("ST", 12, NX, 13))
-        ts(V("m7"), V("vi"), 7, A.bitwise_and)
+        fin = V("ST", 12, NX, 13)
+        act(V("rnd"), fin, bias=1532.5)
+        act(V("sg"), fin, F.Sign, bias=0.5)
         if not last:
-            ts(TC, V("ST", 12, NX, 13), 0.0, A.is_ge, 96.0, A.mult)
-            tt(V("oSL%d" % (t + 1)), V("m7"), TC, A.add)
+            mms((PA, V("idn"), fin, True, False), (PA, V("im1"), V("rnd"), False, False), (PA, V("i48"), V("sg"), False, True))
+            act(V("oSL%d" % (t + 1)), PA, bias=1584.0)
             post("SL", t + 1)
+        mms((PB, V("idn"), fin, True, False), (PB, V("im1"), V("rnd"), False, False), (PB, V("im4"), V("sg"), False, True))
+        act(V("sfin"), PB, bias=1540.0)
         ts(TA, V("P0", 0, 192), V("thr", 0, 1), A.is_ge)
         tt(V("kk"), V("KX"), TA, A.mult)
         tree("kk", V("kxi"))
@@ -456,9 +469,9 @@ def rank_program(g, core, T, topo):
         for m in range(6, L): act(blk("am", m), V("sxf"), scale=float(KAP[m]), bias=float(97 * t))
         rep("P0", 192, "xkb")
         rowsum(V("P2", 0, 16), "sel", "wx", 0, 256, 1)
-        ts(TC, V("z"), -3064.5, A.max, -3060.5, A.min)
-        ts(V("p2"), V("z"), ND0 + 256.0 + KZ, A.is_ge, 8.0, A.mult)
-        tt(V("P3", 0, 256), V("p2"), TC, A.subtract)
+        act(V("sn"), V("z"), F.Sign, bias=3062.5)
+        act(V("sf"), V("z"), F.Sign, bias=2938.5)
+        mms((V("P3", 0, 256), V("im2"), V("sn"), True, False), (V("P3", 0, 256), V("i4"), V("sf"), False, True))
         ts(V("kxd0"), V("xkf"), -2048.0, A.mult, 26624.0, A.add)
         tt(V("kxd"), V("kxd0"), V("sxf"), A.add)
         tt(V("eqm"), V("ki"), V("P0", 192, 384), A.is_equal)
@@ -483,24 +496,30 @@ def rank_program(g, core, T, topo):
             cp(blk("cu", h, 64), blk("cj", h, 64))
         rep("P1", 192, "dkb")
         for m in range(L):
-            if m == 2:
+            if m == CFG["sd"]:
                 for k in range(L): act(blk("P5", k), V("sd1"))
-            act(blk("eg", m, 256), IND("E", blk("cu", m)), F.Copy)
+            if m in CFG["ca"]: act(blk("egb", m, 256), IND("E", blk("cu", m)), F.Copy)
+            else: act(blk("eg", m, 256), IND("E", blk("cu", m)), bias=3066.5)
 
         def cadd(h):
             for m in range(4 * h, 4 * h + 4):
-                tt(blk("yc", m, 256), blk("eg", m, 256), V("P3", 0, 256), A.add)
+                if m in CFG["ca"]:
+                    P = (PA, PB)[CFG["ca"].index(m) % 2]
+                    mms((P, V("idn"), blk("egb", m, 256), True, False), (P, V("im2"), V("sn"), False, False), (P, V("i4"), V("sf"), False, True))
+                    act(blk("yc", m, 256), P, bias=3066.5)
+                else: tt(blk("yc", m, 256), blk("eg", m, 256), V("P3", 0, 256), A.add)
             o = blk("P4", h, 64)
-            rowsum(o, "sels", "yc", 1024 * h, 1024 * h + 1024, 1, [(o, V("c512"), V("cm15"), True, False)])
+            rowsum(o, "sels", "yc", 1024 * h, 1024 * h + 1024, 1,
+                   [(o, V("c512"), V("cm15"), True, False), (o, V("idn"), blk("ckm", h, 64), False, False)])
 
-        tt(V("gem"), V("gt"), V("eqm"), A.add)
+        tt(V("gem"), V("ki"), V("P0", 192, 384), A.is_le)
         tt(V("dr0"), V("gt"), SP(16), A.mult)
         tt(TA, V("gem"), SP(), A.mult)
         tt(V("dis"), V("dr0"), TA, A.subtract)
         ts(V("fnd"), V("xkf"), 1.0, A.is_ge)
         if t:
-            cp(V("QF"), V("QU%d" % t))
             cp(QP(), V("QU%d" % t))
+            act(V("QF"), QP())
         tt(V("goq"), V("QF"), V("P5", 0, 192), A.is_equal)
         tt(TB, V("ki"), V("P1", 192, 384), A.is_equal)
         tt(V("go"), V("goq"), TB, A.max)
@@ -508,10 +527,9 @@ def rank_program(g, core, T, topo):
             (V("P2", 256 + 16 * s, 448), V("i4k"), V("go", 0, 192 - 16 * s), False, s == L - 1) for s in range(1, L)]))
         cadd(0)
         ts(V("c1"), V("cj"), 1.0, A.add)
-        tt(V("kadd"), V("cj"), V("ckm"), A.add)
         tt(V("zs"), V("SF"), Z, A.add)
         cadd(1)
-        compact("zs", "asi", CFG["cs"])
+        compact("zs", "asi", CFG["cs"], 0)
         cadd(2)
         ts(V("asj"), V("asi"), 4095, A.bitwise_and)
         ts(TA, V("asj"), 0.0, A.is_equal)
@@ -521,16 +539,16 @@ def rank_program(g, core, T, topo):
         cp(V("ui"), V("P2", 128, 144))
         ts(V("uj"), V("ui"), 7, A.bitwise_and)
         tt(V("uo"), V("lb8"), V("uj"), A.add)
-        ts(TC, V("ST", 12, NX, 13), 0.0, A.is_lt, 8.0, A.mult)
         cp(V("uu"), V("uo"))
-        tt(V("sfin"), V("m7"), TC, A.add)
         tt(V("ev"), IND("E", V("uu")), V("sfin"), A.add)
-        ts(V("enb"), V("ev"), 0.5, A.mult, 159.75, A.add)
-        act(V("en"), V("enb"), bias=-160.0)
+        act(V("enb"), V("ev"), scale=0.5, bias=159.75)
         if not last:
-            act(V("u8"), V("enb"), bias=-168.0)
+            act(V("sg"), V("enb"), F.Sign, bias=-171.5)
             act(V("uq"), V("enb"), F.Abs, bias=-167.5)
-        tt(V("kk"), V("kadd"), V("P4", 0, 192), A.add)
+            mms((PB, V("idn"), V("enb"), True, False), (PB, V("im60"), V("sg"), False, True))
+            act(V("uh"), PB, bias=-108.0)
+        act(V("en"), V("enb"), bias=-160.0)
+        tt(V("kk"), V("cj"), V("P4", 0, 192), A.add)
         tree("kk", V("kb"))
         tt(V("pge"), V("kb"), V("bar32"), A.is_ge)
         ts(V("cb"), V("kb"), 2047, A.bitwise_and)
@@ -551,9 +569,7 @@ def rank_program(g, core, T, topo):
             act(V("rj"), V("ret"), F.Copy, acc=V("rc", 0, 1))
             act(V("rcb", 0, 1), V("rc", 0, 1), F.Copy)
             mms((V("P2", 64, 65), V("ones"), V("rcb", 0, 1), True, True))
-            ts(TC, V("enb"), 172.0, A.is_lt, 120.0, A.mult)
             ts(V("um"), V("uq"), 4.0, A.is_ge)
-            tt(V("uh"), V("u8"), TC, A.add)
             tt(IND("X8", V("uu")), V("uh"), V("um"), A.mult)
             cp(IND("E", V("uu")), V("en"))
         else:
@@ -562,7 +578,7 @@ def rank_program(g, core, T, topo):
             cp(IND("E", V("uu")), V("en"))
             store("out2", T.ye[:, :], V("E"))
         tt(V("zq"), V("QF"), Z, A.add)
-        compact("zq", "aqi", CFG["cq"])
+        compact("zq", "aqi", CFG["cq"], 3)
         tt(V("drq"), V("gt"), QP(16), A.mult)
         tt(TA, V("gem"), QP(), A.mult)
         ts(V("aqj"), V("aqi"), 4095, A.bitwise_and)

import math
import numpy as np
from concourse.mybir import AluOpType as A, ActivationFunctionType as F

N, W, L, VI = 8, 2048, 12, 4
PLAN_STEP, STATE_STEP = 5, 1
KAP = [149 * m + 37 for m in range(L)]
NX = 13 * 256
ND0, NDO = 98304.0, 248.5
KZ = -3064.5 - ND0 - 130.0
LNB = 9 * math.log(2.0)
THR0 = 16 * ND0

BUFS = {"bfloat16": {}, "float32": {}, "int32": {}, "uint16": {}}
ARENA = {"bfloat16": {}, "float32": {}, "int32": {}, "uint16": {}}
for _n in "E X8 PT t120 e8 qa mm nb0 sel sels".split():
    BUFS["bfloat16"][_n] = W
for _n in "Gb NB ST".split():
    BUFS["bfloat16"][_n] = NX
for _n in "Yb egb yc ng".split():
    BUFS["bfloat16"][_n] = 3072
MULT = [("i4k", 4096.0), ("i64k", 65536.0), ("i249", 249.0), ("im1", -1.0), ("i48", 48.0), ("im4", -4.0), ("im2", -2.0), ("i4", 4.0), ("im60", -60.0)]
for _n in "ones idn bd1 bd c512".split() + [_m[0] for _m in MULT]:
    BUFS["bfloat16"][_n] = 128
BUFS["float32"]["ND"] = W
BUFS["float32"]["eg"] = 3072
for _n, _w in (("actl", 192), ("whyl", 192), ("barl", 16)):
    BUFS["int32"][_n] = _w
BUFS["bfloat16"]["stl"] = 256
BUFS["float32"]["ysf"] = BUFS["float32"]["ywf"] = 192
for _n in "c0t c8t wx sfin enb en uq um uh rnd sg sn sf".split():
    ARENA["bfloat16"][_n] = 256
for _n, _w in (("cm15", 64), ("ckm", 192), ("go", 192), ("xkb", 16), ("dkb", 16), ("shb", 16), ("slb", 16), ("put", 16), ("ret", 16), ("rj", 16), ("rcb", 16)):
    ARENA["bfloat16"][_n] = _w
for _n in "SF QF".split():
    ARENA["float32"][_n] = 192
for _n in ("ki ckx ckd KX KD kk am dk0 goq zs zq tlc dr dr0 drq dis diq eqm gt gem c1 na nc qa1 qc1 sa0 sa1 sa2").split():
    ARENA["float32"][_n] = 192
for _n in "stx z ev".split():
    ARENA["float32"][_n] = 256
for _n, _w in (("k2", 96), ("k3", 48)):
    ARENA["float32"][_n] = _w
for _n in "k4 lb lb13 lb8 bar32 thr xkf sxf posf kxd kxd0 bx wf sd1 fnd pge uo rc".split():
    ARENA["float32"][_n] = 16
for _n in "asi asj aqi aqj ci cj".split():
    ARENA["int32"][_n] = 192
ARENA["int32"]["p5r"] = 64
for _n in "pi bi kxi xk sxi di d1 sdi sh sl pr kb cb ui uj ri rj1".split():
    ARENA["int32"][_n] = 16
for _n, _w in (("sxu", 16), ("posu", 16), ("uu", 16), ("cu", 192), ("SU0", 192)):
    ARENA["uint16"][_n] = _w
for _t in (1, 2, 3):
    for _n, _w, _d in (("SU", 192, "uint16"), ("QU", 192, "uint16"), ("SL", 256, "bfloat16")):
        BUFS[_d]["%s%d" % (_n, _t)] = _w
        BUFS[_d]["o%s%d" % (_n, _t)] = _w
SCRATCH, WID, PLACE = {}, {}, {}
for _d in BUFS:
    for _n in BUFS[_d]:
        WID[_n] = BUFS[_d][_n]
        PLACE[_n] = (_n, 0, WID[_n])
    _a, _o = "ar_" + _d, 0
    for _n in ARENA[_d]:
        PLACE[_n] = (_a, _o, ARENA[_d][_n])
        _o += ARENA[_d][_n]
    WID[_a] = _o
    for _n in list(BUFS[_d]) + [_a]:
        SCRATCH[_n] = ("sbuf", [128, WID[_n]], _d)
PS = ["P%d" % i for i in range(8)]
for _n in PS:
    WID[_n] = 512
    PLACE[_n] = (_n, 0, 512)
    SCRATCH[_n] = ("psum", [128, 512], "float32")
MSG = ["SL", "SU", "QU"]
LOADS = ["actl", "whyl", "barl", "stl", "PT", "E0", "E1", "E2", "E3"]
SEMAPHORES = ["sv", "sa", "st", "sg", "loc", "rel"] + ["ld" + n for n in LOADS] + ["out0", "out1", "out2"] \
    + ["a%s%d" % (n, t) for n in MSG for t in (1, 2, 3)] + ["h%s%d" % (n, t) for n in MSG for t in (1, 2, 3)]

CFG = {"xdve": [2, 4, 4, 4], "fa": [1, 4, 7, 10], "ca": [], "cs": list(range(4, 12)), "sd": 2, "late": {"SL": 10.0, "SU": 0.5, "QU": 5.0}, "cq": list(range(1, 12)), "wake": 0.15, "eps": 0.05}
PLAN = {}


def route(T, topo, p, kind):
    src = T.cores[p]
    dst = T.cores[(p + (STATE_STEP if kind == "SL" else PLAN_STEP)) % N]
    plan = T.cores[(p + PLAN_STEP) % N]
    if topo.may_write(src, dst) and topo.may_write(src, plan):
        return src, dst, None
    if topo.may_write(src, dst) and kind != "SL":
        return src, dst, None
    hs = [h for h in topo.cores_of(src) if h != src and topo.may_write(h, dst) and topo.may_write(h, plan)]
    hs.sort(key=lambda h: topo.die(h) != topo.die(src))
    return src, dst, hs[0]


def send(g, T, topo, src, dst, out, inp, rsem, lsem, final):
    rid, pid = topo.addr(dst, src)
    m = topo.mask(src, dst) & topo.mask(dst if dst != final else src, final)
    g.remote_dma(out_ap=out, in_ap=inp, remote_sem=T.sem[rsem], local_sem=T.sem[lsem], pid=pid, routing_id=rid, dma_engine_mask=m)
    return count(topo, src, dst, final)


def count(topo, src, dst, final):
    return len([e for e in topo.engines(src, dst) if e in topo.engines(dst if dst != final else src, final)])


def helper_program(g, core, T, topo):
    jobs = []
    for t in (1, 2, 3):
        for kind in MSG:
            for p in range(N):
                src, dst, h = route(T, topo, p, kind)
                if h == core:
                    jobs.append((t, kind, src, dst))
    n = 0
    for t, kind, src, dst in jobs:
        g.wait_ge(T.sem["h%s%d" % (kind, t)], count(topo, src, core, dst))
        b = "%s%d" % (kind, t)
        n += send(g, T, topo, core, dst, T[b][:], T["o" + b][:], "a" + b, "rel", dst)
    if n:
        g.wait_ge(T.sem["rel"], n)


def rank_program(g, core, T, topo):
    rank = T.rank_of(core)
    if rank is None:
        helper_program(g, core, T, topo)
        return
    eng = {"sv": g.vector, "sa": g.scalar, "st": g.tensor, "sg": g, "sync": g.sync}
    banks = set(PS)
    ops = []
    hist = {}

    def meet(a, b):
        if a[1] >= b[2] or b[1] >= a[2]: return False
        return a[3] != b[3] or a[3] == 1 or (a[1] - b[1]) % a[3] == 0

    def emit(q, fns, reads, writes, cost=0.08, sem=None, inc=1, lat=0.0, after=()):
        n, pred = len(ops), set(after)
        for vs, wrt in ((reads, False), (writes, True)):
            for v in vs:
                bank = v[0] in banks
                h = hist.setdefault(v[0] if bank else v[4], [])
                for i, u, w in h:
                    if (bank and ops[i][0] != q) or ((w or wrt) and meet(u, v)): pred.add(i)
                if wrt and v[3] == 1:
                    h[:] = [e for e in h if not (v[1] <= e[1][1] and e[1][2] <= v[2] and (not bank or ops[e[0]][0] == q))]
        ops.append([q, fns if isinstance(fns, list) else [fns], pred, cost, sem or q, inc, lat])
        for vs, wrt in ((reads, False), (writes, True)):
            for v in vs:
                hist[v[0] if v[0] in banks else v[4]].append((n, v, wrt))
        return n

    def schedule():
        n = len(ops)
        succ = [[] for _ in range(n)]
        for i, o in enumerate(ops):
            for p in o[2]: succ[p].append(i)
        prio = [0.0] * n
        for i in range(n - 1, -1, -1):
            o = ops[i]
            prio[i] = o[3] + o[6] + max([prio[j] + CFG["wake"] for j in succ[i]] + [0.0])
        left = [len(o[2]) for o in ops]
        ready = [0.0] * n
        free = {}
        pool = {}
        order = []
        for i in range(n):
            if not left[i]: pool.setdefault(ops[i][0], []).append(i)
        while len(order) < n:
            best = None
            for q in pool:
                if not pool[q]: continue
                f = free.get(q, 0.0)
                lo = min(max(f, ready[i]) for i in pool[q])
                i = max((j for j in pool[q] if max(f, ready[j]) <= lo + CFG["eps"]), key=lambda j: (prio[j], -j))
                st = max(f, ready[i])
                if best is None or st < best[0]: best = (st, i, q)
            st, i, q = best
            pool[q].remove(i)
            order.append(i)
            o = ops[i]
            if q != "arr": free[q] = st + o[3]
            for j in succ[i]:
                ready[j] = max(ready[j], st + o[3] + o[6] + CFG["wake"])
                left[j] -= 1
                if not left[j]: pool.setdefault(ops[j][0], []).append(j)
        return order

    def issue(order):
        cnt, tok, snap = {}, {}, {}
        known = {q: {} for q in eng}
        for i in order:
            q, fns, pred, _c, s, inc, _l = ops[i]
            if q == "arr":
                tok[i] = (s, inc)
                cnt[s] = inc
                continue
            k = known[q]
            w = {}
            for p in pred:
                if q == "st" and ops[p][0] == "st": continue
                if tok[p]: w[tok[p][0]] = max(w.get(tok[p][0], 0), tok[p][1])
            for z in sorted(w):
                for y in w:
                    if y != z and snap.get((y, w[y]), {}).get(z, 0) >= w[z] and k.get(z, 0) < w[z] and k.get(y, 0) < w[y]:
                        break
                else:
                    if k.get(z, 0) < w[z]: eng[q].wait_ge(T.sem[z], w[z])
            for z in w:
                k[z] = max(k.get(z, 0), w[z])
                for s2, c2 in snap.get((z, w[z]), {}).items():
                    if k.get(s2, 0) < c2: k[s2] = c2
            for f in fns[:-1]: f(eng[q])
            r = fns[-1](eng[q])
            tok[i] = None
            if s != "none":
                r.then_inc(T.sem[s], inc)
                cnt[s] = cnt.get(s, 0) + inc
                tok[i] = (s, cnt[s])
                snap[tok[i]] = dict(k)
        for z in sorted(cnt):
            if known["sg"].get(z, 0) < cnt[z]: g.wait_ge(T.sem[z], cnt[z])

    def V(n, lo=0, hi=None, step=1):
        b, o, w = PLACE[n]
        return (b, o + lo, o + (w if hi is None else hi), step, n)

    def IND(win, off):
        return ("ind", win, off)

    def ap(v):
        if len(v) == 3: return T[v[1]][:, 0:WID[v[1]]].indirect(ap(v[2]))
        return T[v[0]][:, v[1]:v[2]:v[3]] if v[3] != 1 else T[v[0]][:, v[1]:v[2]]

    def rl(*vs):
        o = []
        for v in vs:
            if isinstance(v, tuple):
                o += [V(v[1]), v[2]] if len(v) == 3 else [v]
        return o

    def sc(x):
        return ap(x) if isinstance(x, tuple) else x

    def el(v):
        return 16 * el(v[2]) if len(v) == 3 else -(-(v[2] - v[1]) // v[3])

    CY = 0.00083 * 1.2

    def price(out, ins, per, ind=0.05):
        if len(out) == 3: return ind + el(out) * 3.5 * CY
        if any(len(i) == 3 for i in ins): return ind + el(out) * 1.5 * CY
        return max(64, el(out) * per) * CY

    def two(*vs):
        return all(len(v) == 5 and v[0] not in banks and SCRATCH[v[0]][2] in ("bfloat16", "uint16") for v in vs)

    def ts(out, i0, s1, op0, s2=None, op1=None):
        if op1 is None: f = lambda e: e.tensor_scalar(ap(out), ap(i0), sc(s1), None, op0)
        else: f = lambda e: e.tensor_scalar(ap(out), ap(i0), sc(s1), sc(s2), op0, op1)
        emit("sv", f, rl(i0, s1, s2), [out], price(out, [i0], 0.5 if two(out, i0) else 1))

    def tt(out, i0, i1, op):
        f = lambda e: e.tensor_tensor(ap(out), ap(i0), ap(i1), op)
        c = price(out, [i0], 1 if i0[0] in banks or i1[0] in banks else 2)
        if len(out) == 3: emit("sv", f, rl(i0, i1, out[2]), [V(out[1])], c)
        else: emit("sv", f, rl(i0, i1), [out], c)

    def cp(out, i0):
        f = lambda e: e.tensor_copy(ap(out), ap(i0))
        c = price(out, [i0], 0.5 if two(out, i0) else 1)
        if len(out) == 3: emit("sv", f, rl(i0, out[2]), [V(out[1])], c)
        else: emit("sv", f, rl(i0), [out], c)

    def ms(out, c):
        emit("sv", lambda e: e.memset(ap(out), c), [], [out], price(out, [], 0.5 if two(out) else 1))

    def act(out, i0, func=F.Identity, scale=1.0, bias=0.0, acc=None):
        if acc is None: f = lambda e: e.activation(ap(out), ap(i0), func, bias=bias, scale=scale)
        else: f = lambda e: e.activation(ap(out), ap(i0), func, bias=bias, scale=scale, accum_out=ap(acc))
        emit("sa", f, rl(i0), [out] + ([acc] if acc else []), price(out, [i0], 1, 0.065))

    def mms(*jobs):
        fs = [lambda e, j=j: e.matmul(ap(j[0]), ap(j[1]), ap(j[2]), j[3], j[4]) for j in jobs]
        emit("st", fs, [v for j in jobs for v in (j[1], j[2])], [j[0] for j in jobs], sum(max(64, el(j[2])) * (1 if two(j[2]) else 4) for j in jobs) * CY)

    def load(q, sem, out, src):
        emit(q, lambda e: e.dma_start(ap(out), src), [], [out], sem="ld" + sem, inc=16, lat=2.5)

    def store(sem, dst, src):
        emit("sync", lambda e: e.dma_start(dst, ap(src)), [src], [], sem=sem, inc=16, lat=2.5)

    def rowsum(out, selb, buf, lo, hi, step, before=()):
        mms(*(list(before) + [(out, V(selb, 128 * j, 128 * j + 128), V(buf, lo + j * step, hi, 16 * step),
                               not before and j == 0, j == 15) for j in range(16)]))

    def rep(bank, lo, src):
        mms(*[(V(bank, lo + 16 * k, lo + 16 * k + 16), V("idn"), V(src), True, True) for k in range(L)])

    def tree(src, out, other=None):
        tt(V("k2"), V(src, 0, 96), V(src, 96, 192), A.max)
        tt(V("k3"), V("k2", 0, 48), V("k2", 48, 96), A.max)
        tt(V("k4"), V("k3", 0, 16), V("k3", 16, 32), A.max)
        last = V("k3", 32, 48)
        if other:
            tt(V("wf"), last, other, A.max)
            last = V("wf")
        tt(out, V("k4"), last, A.max)

    def compact(z, acc, scalar, bank):
        ts(V(acc), V(z), 0.0, A.max, 4096.0, A.min)
        ws = [192 - 16 * r for r in range(L)]
        rs = sorted(range(1, L), key=lambda r: (r in scalar, r))

        def spot(r):
            i = rs.index(r) % 2
            return V("P%d" % (bank + i), 0, ws[r]) if r in scalar else V("P7", 192 * i, 192 * i + ws[r])
        for i in range(L):
            if i < L - 1:
                r = rs[i]
                if r in scalar:
                    sa = V("sa%d" % (r % 3), 0, ws[r])
                    act(sa, V(z, 16 * r, 192), F.Relu, bias=-4096.0 * r)
                    act(spot(r), sa, F.Relu, scale=-1.0, bias=4096.0)
                else: ts(spot(r), V(z, 16 * r, 192), 4096.0 * r, A.max, 4096.0 * (r + 1), A.min)
            if i:
                r = rs[i - 1]
                tt(V(acc, 0, ws[r]), V(acc, 0, ws[r]), spot(r), A.subtract if r in scalar else A.add)

    blk = lambda n, k, w=16: V(n, w * k, w * k + w)
    SP = lambda sh=0: V("P6", 16 - sh, 208 - sh)
    QP = lambda sh=0: V("P6", 224 - sh, 416 - sh)
    TA, TB = V("P7", 0, 192), V("P7", 192, 384)
    PA, PB = V("P4", 256, 512), V("P5", 256, 512)
    TD = V("P7", 384, 448)
    Z = V("P2", 256, 448)

    load("sync", "E0", V("E", 0, 512), T.eff[:, 0:512])
    load("sa", "actl", V("actl"), T.act[:, :])
    load("sync", "E1", V("E", 512, 1024), T.eff[:, 512:1024])
    load("sa", "stl", V("stl"), T.st0[:, :])
    load("sync", "E2", V("E", 1024, 1536), T.eff[:, 1024:1536])
    load("sa", "PT", V("PT"), T.req[:, :])
    load("sync", "E3", V("E", 1536, 2048), T.eff[:, 1536:2048])
    load("sync", "whyl", V("whyl"), T.why[:, :])
    load("sync", "barl", V("barl"), T.bar[:, :])
    ms(V("ones"), 1.0)

    def aff(out, src, pattern, op, base, cm):
        emit("sg", lambda e: e.affine_select(ap(V(out)), ap(V(src)), pattern, op, 0.0, base, cm), [V(src)], [V(out)], 0.4)
    aff("idn", "ones", [[-1, 128]], A.is_equal, 0, 1)
    aff("bd1", "ones", [[-16, 8], [0, 16]], A.is_ge, 0, 1)
    aff("bd", "bd1", [[16, 8], [0, 16]], A.is_ge, 15, -1)
    emit("sg", lambda e: e.iota(ap(V("pi")), [[0, 16]], 0, 1), [], [V("pi")])
    emit("sg", lambda e: e.iota(ap(V("bi")), [[16, 16]], 0, 0), [], [V("bi")])
    emit("sg", lambda e: e.iota(ap(V("ki")), [[-1, 12], [0, 16]], 12, 0, allow_small_or_imprecise_dtypes=True), [], [V("ki")])
    ms(V("sel"), 0.0)
    ms(V("c512"), 512.0)
    ms(V("cm15"), -1536.0)
    ms(V("P6", 0, 16), 0.0)
    ms(V("P6", 208, 224), 0.0)
    ms(V("thr"), THR0 + 1024.0)
    ms(V("NB", 0, NX, 13), 0.0)
    for n, c in MULT[:3]: ts(V(n), V("idn"), c, A.mult)
    cp(V("SU0"), V("actl"))
    ts(V("c0t"), V("stl"), 8.0, A.is_lt, 104.0, A.mult)
    ts(V("c8t"), V("stl"), -8.0, A.add)
    for c in range(4):
        sl = (512 * c, 512 * c + 512)
        P = V(PS[2 + c])
        ts(V("t120", *sl), V("E", *sl), 12.0, A.is_lt, 120.0, A.mult)
        act(V("e8", *sl), V("E", *sl), bias=-8.0)
        act(V("qa", *sl), V("E", *sl), F.Abs, bias=-7.5)
        mms((P, V("idn"), V("e8", *sl), True, False), (P, V("idn"), V("t120", *sl), False, True))
        ts(V("mm", *sl), V("qa", *sl), 4.0, A.is_ge)
        tt(V("X8", *sl), V("mm", *sl), P, A.mult)

    def late_setup():
        ts(V("nb0"), V("PT"), 12.0, A.is_ge)
        ts(V("ND"), V("nb0"), NDO, A.mult, ND0, A.add)
        tt(V("Gb", 0, NX, 13), V("c0t"), V("c8t"), A.add)
        ts(V("SF"), V("actl"), 1.0, A.add)
        ts(SP(), V("actl"), 1.0, A.add)
        ts(V("QF"), V("whyl"), 1.0, A.add)
        ts(QP(), V("whyl"), 1.0, A.add)
        ts(V("ckx"), V("ki"), 2048.0, A.mult, -1.0, A.add)
        ts(V("ckd"), V("ki"), -2048.0, A.mult, 26624.0 + 65535.0, A.add)
        ts(V("ckm"), V("ki"), 2048.0, A.mult, -2048.0, A.add)
        for n, c in MULT[3:]: ts(V(n), V("idn"), c, A.mult)
        ts(V("pi"), V("pi"), 15, A.bitwise_and)
        tt(V("lb"), V("pi"), V("bi"), A.add)
        ts(V("lb13"), V("lb"), 13.0, A.mult, 12.0, A.add)
        ts(V("lb8"), V("lb"), 8.0, A.mult)
        for j in range(16):
            cp(V("sel", 129 * j, 128 * j + 128, 16), V("bd", j, 128, 16))
        ts(V("sels"), V("sel"), 2048.0, A.mult)
        ts(V("bar32"), V("barl"), 32768.0, A.mult)

    nloc = [0]

    def post(kind, t):
        b = "%s%d" % (kind, t)
        src, dst, h = route(T, topo, rank, kind)

        def go(e):
            if h is None: nloc[0] += send(g, T, topo, src, dst, T[b][:], T["o" + b][:], "a" + b, "loc", dst)
            else: nloc[0] += send(g, T, topo, src, h, T["o" + b][:], T["o" + b][:], "h" + b, "loc", dst)
        n = emit("sg", go, [V("o" + b)], [], 0.4, sem="none", lat=2.5)
        p2 = (rank - (STATE_STEP if kind == "SL" else PLAN_STEP)) % N
        s2, d2, h2 = route(T, topo, p2, kind)
        emit("arr", [], [], [V(b)], 0.0, sem="a" + b, inc=len(topo.engines(s2 if h2 is None else h2, core)), lat=CFG["late"][kind], after=(n,))

    for t in range(VI):
        last = t == VI - 1
        su = "SU%d" % t
        off = lambda k: V(su, 16 * k, 16 * k + 16)
        fa = CFG["fa"]
        xd = range(L - CFG["xdve"][t], L)
        for k in range(L):
            if k not in xd: act(V("Gb", 1 + k, NX, 13), IND("X8", off(k)), bias=-8.0)
        if t:
            cp(V("Gb", 0, NX, 13), V("SL%d" % t))
            ts(SP(), V(su), 1.0, A.add)
            act(V("SF"), SP())
        else:
            late_setup()
        tt(V("KX"), V("ckx"), SP(), A.add)
        tt(V("KD"), V("ckd"), SP(), A.add)
        for k in xd: ts(V("Gb", 1 + k, NX, 13), IND("X8", off(k)), -8.0, A.add)
        for k in range(L):
            ts(V("NB", 1 + k, NX, 13), V("Gb", 1 + k, NX, 13), -4.5, A.is_lt)
        for k in fa: act(blk("ng", k, 256), IND("nb0", off(k)), F.Copy)
        emit("sv", lambda e: e.tensor_tensor_scan(ap(V("ST")), ap(V("NB")), ap(V("Gb")), 0.0, A.mult, A.add), [V("NB"), V("Gb")], [V("ST")], NX / 2 * CY)
        for k in range(L):
            if k in fa:
                j = fa.index(k)
                P = V(PS[3 + j % 3], 256 * (j // 3), 256 * (j // 3) + 256)
                mms((P, V("i249"), blk("ng", k, 256), True, False), (P, V("idn"), V("ST", k, NX, 13), False, True))
                act(blk("Yb", k, 256), P, bias=ND0 - 0.5)
            else:
                tt(blk("Yb", k, 256), IND("ND", off(k)), V("ST", k, NX, 13), A.add)
        for q in range(3): rowsum(blk("P0", q, 64), "sel", "Yb", 1024 * q, 1024 * q + 1024, 1)
        rowsum(V("P2", 128, 144), "sel", "ST", 12, NX, 13)
        fin = V("ST", 12, NX, 13)
        act(V("rnd"), fin, bias=1532.5)
        act(V("sg"), fin, F.Sign, bias=0.5)
        if not last:
            mms((PA, V("idn"), fin, True, False), (PA, V("im1"), V("rnd"), False, False), (PA, V("i48"), V("sg"), False, True))
            act(V("oSL%d" % (t + 1)), PA, bias=1584.0)
            post("SL", t + 1)
        mms((PB, V("idn"), fin, True, False), (PB, V("im1"), V("rnd"), False, False), (PB, V("im4"), V("sg"), False, True))
        act(V("sfin"), PB, bias=1540.0)
        ts(TA, V("P0", 0, 192), V("thr", 0, 1), A.is_ge)
        tt(V("kk"), V("KX"), TA, A.mult)
        tree("kk", V("kxi"))
        ts(V("xk"), V("kxi"), 11, A.logical_shift_right)
        ts(V("sxi"), V("kxi"), 2047, A.bitwise_and)
        tt(V("posf"), V("lb13"), V("xk"), A.subtract)
        cp(V("sxu"), V("sxi"))
        cp(V("posu"), V("posf"))
        cp(V("sxf"), V("sxi"))
        ts(V("stx"), IND("ST", V("posu")), KZ, A.add)
        cp(V("xkf"), V("xk"))
        cp(V("xkb"), V("xk"))
        tt(V("z"), IND("ND", V("sxu")), V("stx"), A.add)
        for m in range(6): act(blk("am", m), V("sxf"), scale=float(KAP[m]), bias=float(97 * t))
        act(V("bx"), V("xkf"), F.Exp, scale=-LNB, bias=11 * LNB)
        act(V("wx"), V("z"), F.Exp, scale=LNB / 8, bias=LNB / 8 * (-104.0 - (ND0 + NDO + KZ)))
        for m in range(6, L): act(blk("am", m), V("sxf"), scale=float(KAP[m]), bias=float(97 * t))
        rep("P0", 192, "xkb")
        rowsum(V("P2", 0, 16), "sel", "wx", 0, 256, 1)
        act(V("sn"), V("z"), F.Sign, bias=3062.5)
        act(V("sf"), V("z"), F.Sign, bias=2938.5)
        mms((V("P3", 0, 256), V("im2"), V("sn"), True, False), (V("P3", 0, 256), V("i4"), V("sf"), False, True))
        ts(V("kxd0"), V("xkf"), -2048.0, A.mult, 26624.0, A.add)
        tt(V("kxd"), V("kxd0"), V("sxf"), A.add)
        tt(V("eqm"), V("ki"), V("P0", 192, 384), A.is_equal)
        tt(V("gt"), V("ki"), V("P0", 192, 384), A.is_lt)
        tt(V("wf"), V("bx"), V("P2", 0, 16), A.mult)
        for k in range(L):
            lim = float(0.5 * 512.0 ** k)
            if k < 7: ts(V("P7", 192 + 16 * k, 208 + 16 * k), V("wf"), lim, A.is_ge)
            else: act(V("P3", 256 + 16 * k, 272 + 16 * k), V("wf"), F.Sign, bias=-lim)
        tt(V("dk0", 0, 112), V("KD", 0, 112), V("P7", 192, 304), A.mult)
        tt(V("dk0", 112, 192), V("KD", 112, 192), V("P3", 368, 448), A.mult)
        tree("dk0", V("di"), V("kxd"))
        ts(V("sdi"), V("di"), 2047, A.bitwise_and)
        tt(V("pr"), V("sxf"), V("sdi"), A.mult)
        ts(V("d1"), V("di"), 11, A.logical_shift_right, 15, A.bitwise_and)
        for j in range(4): ts(blk("p5r", j), V("pr"), 5, A.logical_shift_right)
        ts(V("sd1"), V("sdi"), 1.0, A.add)
        for h in range(3):
            tt(blk("ci", h, 64), blk("am", h, 64), V("p5r"), A.add)
            if h == 0: ts(V("dkb"), V("d1"), -1.0, A.mult, 13.0, A.add)
            ts(blk("cj", h, 64), blk("ci", h, 64), 2047, A.bitwise_and)
            cp(blk("cu", h, 64), blk("cj", h, 64))
        rep("P1", 192, "dkb")
        for m in range(L):
            if m == CFG["sd"]:
                for k in range(L): act(blk("P5", k), V("sd1"))
            if m in CFG["ca"]: act(blk("egb", m, 256), IND("E", blk("cu", m)), F.Copy)
            else: act(blk("eg", m, 256), IND("E", blk("cu", m)), bias=3066.5)

        def cadd(h):
            for m in range(4 * h, 4 * h + 4):
                if m in CFG["ca"]:
                    P = (PA, PB)[CFG["ca"].index(m) % 2]
                    mms((P, V("idn"), blk("egb", m, 256), True, False), (P, V("im2"), V("sn"), False, False), (P, V("i4"), V("sf"), False, True))
                    act(blk("yc", m, 256), P, bias=3066.5)
                else: tt(blk("yc", m, 256), blk("eg", m, 256), V("P3", 0, 256), A.add)
            o = blk("P4", h, 64)
            rowsum(o, "sels", "yc", 1024 * h, 1024 * h + 1024, 1,
                   [(o, V("c512"), V("cm15"), True, False), (o, V("idn"), blk("ckm", h, 64), False, False)])

        tt(V("gem"), V("ki"), V("P0", 192, 384), A.is_le)
        tt(V("dr0"), V("gt"), SP(16), A.mult)
        tt(TA, V("gem"), SP(), A.mult)
        tt(V("dis"), V("dr0"), TA, A.subtract)
        ts(V("fnd"), V("xkf"), 1.0, A.is_ge)
        if t:
            cp(QP(), V("QU%d" % t))
            act(V("QF"), QP())
        tt(V("goq"), V("QF"), V("P5", 0, 192), A.is_equal)
        tt(TB, V("ki"), V("P1", 192, 384), A.is_equal)
        tt(V("go"), V("goq"), TB, A.max)
        mms(*([(Z, V("i64k"), V("go"), True, False)] + [
            (V("P2", 256 + 16 * s, 448), V("i4k"), V("go", 0, 192 - 16 * s), False, s == L - 1) for s in range(1, L)]))
        cadd(0)
        ts(V("c1"), V("cj"), 1.0, A.add)
        tt(V("zs"), V("SF"), Z, A.add)
        cadd(1)
        compact("zs", "asi", CFG["cs"], 0)
        cadd(2)
        ts(V("asj"), V("asi"), 4095, A.bitwise_and)
        ts(TA, V("asj"), 0.0, A.is_equal)
        tt(TA, V("c1"), TA, A.mult)
        tt(V("dr0"), V("asj"), TA, A.add)
        tt(V("dr"), V("dr0"), SP(), A.subtract)
        cp(V("ui"), V("P2", 128, 144))
        ts(V("uj"), V("ui"), 7, A.bitwise_and)
        tt(V("uo"), V("lb8"), V("uj"), A.add)
        cp(V("uu"), V("uo"))
        tt(V("ev"), IND("E", V("uu")), V("sfin"), A.add)
        act(V("enb"), V("ev"), scale=0.5, bias=159.75)
        if not last:
            act(V("sg"), V("enb"), F.Sign, bias=-171.5)
            act(V("uq"), V("enb"), F.Abs, bias=-167.5)
            mms((PB, V("idn"), V("enb"), True, False), (PB, V("im60"), V("sg"), False, True))
            act(V("uh"), PB, bias=-108.0)
        act(V("en"), V("enb"), bias=-160.0)
        tt(V("kk"), V("cj"), V("P4", 0, 192), A.add)
        tree("kk", V("kb"))
        tt(V("pge"), V("kb"), V("bar32"), A.is_ge)
        ts(V("cb"), V("kb"), 2047, A.bitwise_and)
        tt(V("put"), V("pge"), V("fnd"), A.mult)
        for j in range(4): ts(V("P7", 384 + 16 * j, 400 + 16 * j), V("cb"), 1.0, A.add)
        tt(V("ret"), V("fnd"), V("put"), A.subtract)
        rep("P0", 0, "put")
        rep("P1", 0, "ret")
        for j in range(3): tt(V("P7", 64 * j, 64 * j + 64), blk("eqm", j, 64), TD, A.mult)
        tt(V("na"), V("dis"), TA, A.add)
        tt(TB, V("dr"), V("P1", 0, 192), A.mult)
        tt(V("nc"), V("SF"), TB, A.add)
        tt(TA, V("na"), V("P0", 0, 192), A.mult)
        tt(V("na"), V("nc"), TA, A.add)
        if not last:
            ts(V("oSU%d" % (t + 1)), V("na"), -1.0, A.add)
            post("SU", t + 1)
            act(V("rj"), V("ret"), F.Copy, acc=V("rc", 0, 1))
            act(V("rcb", 0, 1), V("rc", 0, 1), F.Copy)
            mms((V("P2", 64, 65), V("ones"), V("rcb", 0, 1), True, True))
            ts(V("um"), V("uq"), 4.0, A.is_ge)
            tt(IND("X8", V("uu")), V("uh"), V("um"), A.mult)
            cp(IND("E", V("uu")), V("en"))
        else:
            ts(V("ysf"), V("na"), -1.0, A.add)
            store("out0", T.ys[:, :], V("ysf"))
            cp(IND("E", V("uu")), V("en"))
            store("out2", T.ye[:, :], V("E"))
        tt(V("zq"), V("QF"), Z, A.add)
        compact("zq", "aqi", CFG["cq"], 3)
        tt(V("drq"), V("gt"), QP(16), A.mult)
        tt(TA, V("gem"), QP(), A.mult)
        ts(V("aqj"), V("aqi"), 4095, A.bitwise_and)
        tt(V("diq"), V("drq"), TA, A.subtract)
        tt(TA, V("eqm"), V("P5", 0, 192), A.mult)
        tt(V("drq"), V("aqj"), QP(), A.subtract)
        tt(V("qa1"), V("diq"), TA, A.add)
        tt(TA, V("qa1"), V("P0", 0, 192), A.mult)
        tt(V("qc1"), V("QF"), TA, A.add)
        tt(TB, V("drq"), V("P1", 0, 192), A.mult)
        tt(V("qa1"), V("qc1"), TB, A.add)
        if not last:
            cp(V("oQU%d" % (t + 1)), V("qa1"))
            post("QU", t + 1)
            cp(V("ri", 0, 1), V("P2", 64, 65))
            ts(V("rj1", 0, 1), V("ri", 0, 1), 1, A.bitwise_and)
            ts(V("thr", 0, 1), V("rj1", 0, 1), 512.0, A.mult, THR0 + 1024.0, A.add)
        else:
            ts(V("ywf"), V("qa1"), -1.0, A.add)
            store("out1", T.yw[:, :], V("ywf"))
    if "order" not in PLAN: PLAN["order"] = schedule()
    issue(PLAN["order"])
    g.wait_ge(T.sem["loc"], nloc[0])
